import numpy as np, ml_dtypes
CORES = [5,29,101,125,133,157,229,253]
N = 8
import mx_ref
BF = ml_dtypes.bfloat16
def decode(q):
    o = []
    for b in range(4):
        e = np.zeros((128, 128, 4), np.float32); e[np.arange(128), np.arange(128), b] = 1
        o.append(mx_ref.matmul(mx_ref.quantize(e.reshape(128, 512).astype(BF)), q))
    return np.stack(o, axis=2).reshape(128, -1)
def cut(t, i, w=512):
    return t[:, w * i:w * i + w]
def f(rng, *shape):
    return mx_ref.flush((rng.standard_normal(shape, dtype=np.float32) * np.exp2(rng.integers(-2, 3, shape[:-1] + (1,)))).astype(BF))
def wide(rng, *shape, cols=0):
    v = rng.standard_normal(shape, dtype=np.float32) * np.exp2(rng.integers(-12, 13, shape)).astype(np.float32)
    if cols: v *= np.repeat(np.exp2(rng.integers(-cols, cols + 1, shape[:-2] + (1, shape[-1] // 4))) * (rng.random(shape[:-2] + (1, shape[-1] // 4)) > 0.0625), 4, axis=-1).astype(np.float32)
    return mx_ref.flush(v.astype(BF))
T, CL, O = 256, 31, 2
def taps(v):
    d = np.zeros((N, 128, 512), BF); d[:, :, :64] = mx_ref.flush(v.astype(np.float32).astype(BF)); return d
def planted(rng, a, *v):
    d = setup_inputs(rng); d["x"] = np.array(d["x"]); t = np.zeros((N, 128, 64))
    for r in range(N):
        rows = rng.permutation(512)[:len(v)]
        for m in range(len(v)):
            p, b = divmod(int(rows[m]), 4)
            d["x"][r, p, b::4] = mx_ref.flush(a[r].astype(BF)); t[r, p, b::4] = v[m][r]
    d["u"] = taps(t); return d
def setup_inputs(rng):
    return {"x": f(rng, N, 128, 4 * T), "u": taps(f(rng, N, 128, 64).astype(np.float32) * np.float32(CL * 0.005)), "w": f(rng, N, 128, 2 * O * 512)}
def setup_inputs_edge(rng):
    a = rng.uniform(-0.25, 0.25, (N, T)); a[:, :CL] = -rng.uniform(0.75, 1.25, (N, CL)); a[:, T - CL:] = rng.uniform(0.75, 1.25, (N, CL))
    return planted(rng, a, rng.uniform(0.5, 1.0, (N, 16)) * CL)
def setup_inputs_halves(rng):
    return planted(rng, rng.choice([-3.0, -1.0, 1.0, 3.0], (N, T)), rng.choice([-2.5, -1.5, -0.5, 0.5, 1.5, 2.5], (N, 16)))
def setup_inputs_last(rng):
    a = rng.choice([-1.0, 1.0], (N, T)); a[:, 0] = -1.0; a[:, T - 1] = 1.0
    return planted(rng, a, np.full((N, 16), CL + 1.0), np.full((N, 16), -1.25))
def setup_inputs_out(rng):
    return planted(rng, np.ones((N, T)), np.tile(np.repeat([-256.0, 256.0], 8), (N, 1)))
def setup_inputs_spread(rng):
    d = setup_inputs(rng); d["x"] = wide(rng, N, 128, 4 * T, cols=8)
    d["u"] = taps(f(rng, N, 128, 64).astype(np.float32) * np.float32(CL * 0.005 * 2.0 ** -10)); return d
def check_inputs(d):
    return ["u"] if (np.asarray(d["u"])[:, :, 64:].astype(np.float32) != 0).any() else []
def reference(x, u, w):
    V = np.concatenate([decode(mx_ref.quantize(x[r])) for r in range(N)], axis=1).reshape(8, 16, N * T, 4)
    y = np.zeros((N, 128, O * T), np.float32)
    for r in range(N):
        o = mx_ref.matmul(mx_ref.quantize(u[r]), mx_ref.quantize(x[r]))[:16]
        o = np.minimum(np.maximum(o, np.float32(-CL)), np.float32(CL))
        n = np.rint(o); fr = o - n
        i = np.clip(r * T + np.arange(T) + n.astype(np.int64), 0, N * T - 1); i1 = np.minimum(i + 1, N * T - 1)
        M = []
        for k in range(2):
            t = np.zeros((8, 16, T, 4), np.float32)
            for g in range(8):
                a, b = V[g][:, i[8 * k + g]], V[g][:, i1[8 * k + g]]
                t[g] = a + fr[8 * k + g][None, :, None] * (b - a)
            M.append(mx_ref.quantize(t.reshape(128, 4 * T).astype(BF)))
        for c in range(O):
            y[r][:, T * c:T * c + T] = mx_ref.matmul(mx_ref.quantize(np.ascontiguousarray(cut(w[r], c))), M[0]) + mx_ref.matmul(mx_ref.quantize(np.ascontiguousarray(cut(w[r], O + c))), M[1])
    return {"y": y}

@@ -1,0 +1,325 @@
+from concourse.bass import DstId, RemoteDMATransfer
+from concourse.mybir import dt, AluOpType, ActivationFunctionType
+
+H, TC, CL, PAD = 32, 256, 31, 8
+OWN, EP = 2 * H, TC
+EC = (16, 0, TC - 16, TC - 32)
+IC = (32, 80, 128, 176)
+DUP = TC + 2 * H
+WN = 2 * (DUP + 2 * H)
+SCRATCH = {
+    "ub": ("sbuf", [128, 2, 8, 4], "bfloat16"),
+    "us": ("sbuf", [128, 2, 8, 16, 4], "bfloat16"),
+    "zt": ("sbuf", [128, 9, 16, 4], "bfloat16"),
+}
+for names, width, kind in (("qp", 384, "q"), ("rq", H, "q"), ("qx", 320, "q"), ("qu", 256, "q"), ("qz", 144, "q"), ("qi qw qm", 512, "q"),
+                           ("sp", 384, "s"), ("rs", H, "s"), ("sx", 320, "s"), ("su", 256, "s"), ("sz", 144, "s"), ("si sw sm", 512, "s"),
+                           ("xe", 512, "b"), ("xp xt", 1024, "b"), ("one eye", 516, "b"), ("wb mt", 2048, "b"),
+                           ("pi b0 b1 b3", 1, "i"), ("nl", 64, "i"), ("fn", 512, "i"), ("z0 z1 hj hf hi he lim", 1, "f"), ("ic", 48, "f"),
+                           ("tab dc eq wl we wz", 64, "f"), ("lv ld", 64, "u"), ("zf gi", 2048, "f"), ("v0 v1", WN, "f"),
+                           ("d0 d1", WN + 2 * PAD, "f"), ("pr", 1024, "f"), ("ys", 512, "f"),
+                           ("pf0 pf1 pl px pv0 pv1 pv2 pv3", 512, "p")):
+    for name in names.split():
+        SCRATCH[name] = ("psum" if kind == "p" else "sbuf", [128, width],
+                         {"q": "float8_e4m3fn_x4", "s": "uint8", "b": "bfloat16", "i": "int32", "u": "uint16"}.get(kind, "float32"))
+SEMAPHORES = ("d_xe d_u d_x d_w st1 st2 ra rb arr loc g_p g_e g_c v_ones v_xp v_zt v_hz v_c1 v_c2 v_c3 v_c4 v_tab v_e v_qe v_u1 v_u2 v_u3 "
+              "v_qu v_qp v_qx v_qz v_xi v_n0 v_n1 v_f0 v_f1 v_dc v_eq v_nl v_wl v_we v_wz v_lv v_ld v_qw v_p v_sa v_sb v_ma v_mb v_qa v_qb "
+              "v_pe v_se v_me v_qme v_y s_z s_zt s_xe s_xi s_fi s_fe s_vd s_dd s_va s_vb s_ga s_gb s_vg s_ge s_y s_ye t_f0 t_f1 t_l t_oa0 "
+              "t_oa1 t_ob0 t_ob1 t_oe0 t_oe1").split() + [p + str(b) for p in ("s_v", "s_lv", "v_d", "v_dl", "t_v", "t_lv") for b in range(4)]
+
+
+def mask_of(engines):
+    return sum(1 << e for e in engines)
+
+
+def routes(T, topo, core):
+    r, n = T.rank_of(core), len(T.cores)
+    out = []
+    for side, nb in ((0, r - 1), (1, r + 1)):
+        if not 0 <= nb < n:
+            continue
+        dst = T.cores[nb]
+        cand = [c for c in topo.cores_of(core) if c != core and topo.may_write(c, dst)]
+        cand.sort(key=lambda c: (topo.die(c) != topo.die(core), c))
+        relay = cand[side]
+        out.append((side, relay, dst, topo.engines(core, relay)[4 * side:4 * side + 4], topo.engines(relay, dst)[::2], EP + H * side,
+                    H if side == 1 or nb == 0 else 0))
+    return out
+
+
+def relay_program(g, core, T, topo):
+    for rc in topo.cores_of(core):
+        if T.rank_of(rc) is None:
+            continue
+        for side, relay, dst, near, far, col, land in routes(T, topo, rc):
+            if relay != core:
+                continue
+            rid, pid = topo.addr(dst, core)
+            m = mask_of(far)
+            g.wait_ge(T.sem.ra, len(near))
+            g.remote_dma(T.qx[:, land:land + H].bitcast(dt.uint8), T.rq[:, 0:H].bitcast(dt.uint8), T.sem.arr, T.sem.loc, pid, rid, m)
+            g.wait_ge(T.sem.rb, len(near))
+            g.remote_dma(T.sx[:, land:land + H], T.rs[:, 0:H], T.sem.arr, T.sem.loc, pid, rid, m)
+            g.wait_ge(T.sem.loc, 2 * len(far))
+
+
+def rank_program(g, core, T, topo):
+    rank = T.rank_of(core)
+    if rank is None:
+        relay_program(g, core, T, topo)
+        return
+    n = len(T.cores)
+    first, last = rank == 0, rank == n - 1
+    end = first or last
+    S, A, CP = T.sem, AluOpType, ActivationFunctionType.Copy
+    V, C, P, Y = g.vector, g.scalar, g.tensor, g.sync
+    pv = [T["pv%d" % b] for b in range(4)]
+    pf, vw, dw, TO = [T.pf0, T.pf1], [T.v0, T.v1], [T.d0, T.d1], (1, 3, 0, 2)
+    out = routes(T, topo, core)
+
+    def waits(q, *pairs):
+        for name in pairs:
+            a, _, c = name.partition(":")
+            q.wait_ge(S[a], int(c or 1))
+
+    def group(call, to, cols, src, at, *more):
+        return call(T.xp[:, 4 * to:4 * (to + cols)], src[:, 4 * at:4 * (at + cols)], *more)
+    arrivals = sum(2 * len(q[4]) for nb in (rank - 1, rank + 1) if 0 <= nb < n for q in routes(T, topo, T.cores[nb]) if q[2] == core)
+    Y.dma_start(T.xe[:, 0:4 * H], T.x[:, 0:4 * H]).then_inc(S.d_xe, 16)
+    C.dma_start(T.xe[:, 4 * H:8 * H], T.x[:, 4 * (TC - H):4 * TC]).then_inc(S.d_xe, 16)
+    Y.dma_start(T.ub[:], T.u[:, 0:64]).then_inc(S.d_u, 16)
+    Y.dma_start(T.xt[:], T.x[:]).then_inc(S.d_x, 16)
+    Y.wait_ge(S.d_x, 16)
+    Y.dma_start(T.wb[:], T.w[:]).then_inc(S.d_w, 16)
+    g.iota(T.pi[:], [[0, 1]], 0, 1).then_inc(S.g_p, 1)
+    g.wait_ge(S.v_ones, 1)
+    g.affine_select(T.eye[:], T.one[:], [[-1, 516]], A.is_equal, 0.0, 4, 4).then_inc(S.g_e, 1)
+    g.iota(T.ic[:], [[1, 48]], 0, 0, allow_small_or_imprecise_dtypes=True).then_inc(S.g_c, 1)
+    g.wait_ge(S.v_qe, 1)
+    codes, planes = [], []
+    for side, relay, dst, near, far, col, land in out:
+        rid, pid = topo.addr(relay, core)
+        to = [DstId(rid=rid, pnc=pid)]
+        codes.append(RemoteDMATransfer(dst_ids=to, dma_engine_mask=mask_of(near), remote_sem=S.ra,
+                                       src=T.qp[:, col:col + H].bitcast(dt.uint8), dst=T.rq[:, 0:H].bitcast(dt.uint8)))
+        planes.append(RemoteDMATransfer(dst_ids=to, dma_engine_mask=mask_of(near), remote_sem=S.rb,
+                                        src=T.sp[:, col:col + H], dst=T.rs[:, 0:H]))
+    g.remote_dma_fused(codes, local_sem=S.loc)
+    g.remote_dma_fused(planes, local_sem=S.loc)
+    g.wait_ge(S.loc, sum(2 * len(q[3]) for q in out))
+    V.memset(T.one[:], 1.0).then_inc(S.v_ones, 1)
+    V.memset(T.xe[:, 8 * H:512], 0.0).then_inc(S.v_xp, 1)
+    V.memset(T.zt[:], 0.0).then_inc(S.v_zt, 1)
+    hz = 6 if end else 2
+    for i in range(2):
+        V.memset(dw[i][:, 0:2 * PAD], 0.0).then_inc(S.v_hz, 1)
+        if end:
+            a, e = (TC + H - 1, DUP) if first else (TC - 1, TC + H)
+            V.memset(vw[i][:, 2 * a + 2:2 * e], 0.0).then_inc(S.v_hz, 1)
+            V.memset(dw[i][:, 2 * (a + PAD):2 * (e + PAD)], 0.0).then_inc(S.v_hz, 1)
+    waits(V, "g_p")
+    for b, bit in ((T.b0, 1), (T.b1, 2), (T.b3, 8)):
+        V.tensor_scalar(b[:], T.pi[:], bit, None, A.bitwise_and).then_inc(S.v_c1, 1)
+    waits(V, "v_c1:3")
+    V.tensor_scalar(T.z0[:], T.b0[:], 0.5, float(PAD), A.mult, A.add).then_inc(S.v_c2, 1)
+    V.tensor_scalar(T.z1[:], T.b0[:], 0.5, float(PAD + TC - 1 + 1000), A.mult, A.add).then_inc(S.v_c2, 1)
+    waits(V, "v_c2:2")
+    V.tensor_scalar(T.hj[:], T.b1[:], 24.0, T.z0[:], A.mult, A.add).then_inc(S.v_c3, 1)
+    V.tensor_scalar(T.hf[:], T.b1[:], -8.0, T.z0[:], A.mult, A.add).then_inc(S.v_c3, 1)
+    V.tensor_scalar(T.lim[:], T.b3[:], -125.0, T.z1[:], A.mult, A.add).then_inc(S.v_c4, 1)
+    waits(V, "v_c3:2")
+    V.tensor_scalar(T.hi[:], T.b3[:], 12.0, T.hj[:], A.mult, A.add).then_inc(S.v_c4, 1)
+    V.tensor_scalar(T.he[:], T.b3[:], 28.0 if first else -12.0, T.hf[:], A.mult, A.add).then_inc(S.v_c4, 1)
+
+    def eyes(bs):
+        for b in bs:
+            V.quantize_mx(T.qi[:, 128 * b:128 * b + 128], T.si[:, 128 * b:128 * b + 128], T.eye[:, 4 - b:516 - b]).then_inc(S.v_e, 1)
+    waits(V, "g_e")
+    eyes((1, 3))
+    waits(V, "v_xp", "d_xe:32")
+    V.quantize_mx(T.qp[:, EP:EP + 128], T.sp[:, EP:EP + 128], T.xe[:]).then_inc(S.v_qe, 1)
+    waits(V, "d_u:16")
+    for q in range(4):
+        V.tensor_copy(T.us[:, :, :, q, :], T.ub[:]).then_inc(S.v_u1, 1)
+    eyes((0,))
+    waits(V, "v_u1:4")
+    V.tensor_copy(T.us[:, :, :, 4:8, :], T.us[:, :, :, 0:4, :]).then_inc(S.v_u2, 1)
+    eyes((2,))
+    waits(V, "v_u2")
+    V.tensor_copy(T.us[:, :, :, 8:16, :], T.us[:, :, :, 0:8, :]).then_inc(S.v_u3, 1)
+    waits(V, "d_x:16")
+    V.quantize_mx(T.qx[:, OWN:OWN + TC], T.sx[:, OWN:OWN + TC], T.xt[:]).then_inc(S.v_qx, 1)
+    for h in (2, 3):
+        group(V.tensor_copy, 64 * h + 16, 48, T.xt, IC[h]).then_inc(S.v_xi, 1)
+    waits(V, "v_u3")
+    V.quantize_mx(T.qu[:], T.su[:], T.us[:]).then_inc(S.v_qu, 1)
+    waits(V, "v_xi:2", "s_xe:4", "s_xi:2")
+    V.quantize_mx(T.qp[:, 0:TC], T.sp[:, 0:TC], T.xp[:]).then_inc(S.v_qp, 1)
+    waits(V, "s_zt:4")
+    V.quantize_mx(T.qz[:], T.sz[:], T.zt[:]).then_inc(S.v_qz, 1)
+    waits(V, "v_c4:3", "g_c")
+    V.tensor_scalar(T.tab[:, 0:16], T.ic[:, 0:16], T.he[:], float(EC[0] + (0 if first else DUP)), A.add, A.add).then_inc(S.v_tab, 1)
+    V.tensor_scalar(T.tab[:, 16:64], T.ic[:], T.hi[:], float(IC[0]), A.add, A.add).then_inc(S.v_tab, 1)
+
+    def own_d(t):
+        waits(V, "s_v%d" % t)
+        V.tensor_tensor(dw[t % 2][:, 2 * PAD + t // 2:2 * (PAD + TC - 1):2], pv[t][:, 1:TC],
+                        vw[t % 2][:, t // 2:2 * (TC - 1):2], A.subtract).then_inc(S["v_d%d" % t], 1)
+
+    def fr(k):
+        waits(V, "v_n%d" % k)
+        for h in range(4):
+            q = 4 * k + 2 * (h % 2) + 8 * (h // 2)
+            a = 256 * k + 64 * h
+            V.tensor_tensor(T.zf[:, 2 * q + 1:2048:32], pf[k][:, 64 * h:64 * h + 64], T.fn[:, a:a + 64],
+                            A.subtract).then_inc(S["v_f%d" % k], 1)
+    own_d(1)
+    own_d(3)
+    for k in range(2):
+        waits(V, "t_f%d" % k)
+        V.tensor_scalar(T.fn[:, TC * k:TC * k + TC], pf[k][:, 0:TC], -float(CL), float(CL), A.max, A.min).then_inc(S["v_n%d" % k], 1)
+    fr(0)
+    waits(V, "t_l")
+    V.tensor_scalar(T.dc[:], T.pl[:, 0:64], -float(CL), float(CL), A.max, A.min).then_inc(S.v_dc, 1)
+    fr(1)
+    waits(V, "v_dc")
+    V.tensor_copy(T.nl[:], T.dc[:]).then_inc(S.v_nl, 1)
+    V.tensor_tensor(T.eq[:], T.dc[:], T.pl[:, 0:64], A.is_equal).then_inc(S.v_eq, 1)
+    waits(V, "v_tab:2", "v_nl")
+    V.tensor_tensor(T.wl[:], T.nl[:], T.tab[:], A.add).then_inc(S.v_wl, 1)
+    own_d(0)
+    waits(V, "v_wl", "v_eq")
+    wl = T.wl
+    if end:
+        wl = T.we
+        V.tensor_scalar(T.we[:], T.wl[:], T.z0[:] if first else T.lim[:], None, A.max if first else A.min).then_inc(S.v_we, 1)
+        waits(V, "v_we")
+    V.tensor_tensor(T.wz[:], wl[:], T.eq[:], A.mult).then_inc(S.v_wz, 1)
+    V.tensor_scalar(T.lv[:], wl[:], 2.0, -2.0 * PAD, A.mult, A.add).then_inc(S.v_lv, 1)
+    own_d(2)
+    waits(V, "v_wz")
+    V.tensor_scalar(T.ld[:], T.wz[:], 2.0, None, A.mult).then_inc(S.v_ld, 1)
+    di, vi = 2 * (PAD + TC - 1), 2 * (TC - 1)
+    waits(V, "v_ld", "v_lv", "s_fi", "v_hz:%d" % hz, "v_d0", "v_d2")
+    V.tensor_tensor(T.pr[:, 256:1024], T.d0[:, 0:di].indirect(T.ld[:, 16:64]), T.zf[:, 513:2048:2], A.mult).then_inc(S.v_p, 1)
+    waits(V, "d_w:16")
+    V.quantize_mx(T.qw[:], T.sw[:], T.wb[:]).then_inc(S.v_qw, 1)
+    waits(V, "s_z:2")
+    halves = ((16, 40, "a"), (40, 64, "b"))
+    for m0, m1, c in halves:
+        waits(V, "s_v" + c, "s_g" + c)
+        V.tensor_tensor_scan(T.mt[:, 32 * m0:32 * m1], T.zf[:, 32 * m0:32 * m1], T.gi[:, 32 * m0:32 * m1], 0.0,
+                             A.mult, A.add).then_inc(S["v_s" + c], 1)
+    waits(V, "v_p")
+    for m0, m1, c in halves:
+        waits(V, "v_s" + c)
+        V.tensor_tensor(T.mt[:, 32 * m0:32 * m1:2], T.v0[:, 0:vi].indirect(T.lv[:, m0:m1]), T.pr[:, 16 * m0:16 * m1],
+                        A.add).then_inc(S["v_m" + c], 1)
+    for m0, m1, c in halves:
+        waits(V, "v_m" + c)
+        V.quantize_mx(T.qm[:, 8 * m0:8 * m1], T.sm[:, 8 * m0:8 * m1], T.mt[:, 32 * m0:32 * m1]).then_inc(S["v_q" + c], 1)
+    a, e, b = (TC + H, DUP, 1) if last else (TC - 1, TC + H - 1 if first else DUP, 0)
+    for t in TO:
+        waits(V, "s_lv%d" % t)
+        V.tensor_tensor(dw[t % 2][:, 2 * (PAD + a) + t // 2:2 * (PAD + e):2], pv[t][:, b:b + e - a],
+                        vw[t % 2][:, 2 * a + t // 2:2 * e:2], A.subtract).then_inc(S["v_dl%d" % t], 1)
+    waits(V, "s_dd:2", "s_vd:2", "s_fe", "v_dl0", "v_dl2")
+    V.tensor_tensor(T.pr[:, 0:256], T.d0[:].indirect(T.ld[:, 0:16]), T.zf[:, 1:512:2], A.mult).then_inc(S.v_pe, 1)
+    waits(V, "s_vg", "s_ge")
+    V.tensor_tensor_scan(T.mt[:, 0:512], T.zf[:, 0:512], T.gi[:, 0:512], 0.0, A.mult, A.add).then_inc(S.v_se, 1)
+    waits(V, "v_pe", "v_se")
+    V.tensor_tensor(T.mt[:, 0:512:2], T.v0[:].indirect(T.lv[:, 0:16]), T.pr[:, 0:256], A.add).then_inc(S.v_me, 1)
+    waits(V, "v_me")
+    V.quantize_mx(T.qm[:, 0:128], T.sm[:, 0:128], T.mt[:, 0:512]).then_inc(S.v_qme, 1)
+
+    def edge_y(call, o, src, sem):
+        for h in range(4):
+            call(T.ys[:, TC * o + EC[h]:TC * o + EC[h] + 16], src[:, h % 2 + 4 * (h // 2):128:8]).then_inc(sem, 1)
+    waits(V, "t_oe1")
+    edge_y(V.tensor_copy, 1, T.px, S.v_y)
+
+    def mm(o, cols, lq, ls, a, rq, rs, c, start, stop):
+        return P.matmul_mx(o[:, 0:cols], lq[:, a:a + 128], ls[:, a:a + 128], rq[:, c:c + cols], rs[:, c:c + cols], start, stop)
+    waits(P, "v_e:4", "v_qx")
+    for t in TO:
+        mm(pv[t], TC, T.qi, T.si, 128 * t, T.qx, T.sx, OWN, True, True).then_inc(S["t_v%d" % t], 1)
+    waits(P, "v_qu", "v_qp")
+    for k in range(2):
+        mm(pf[k], TC, T.qu, T.su, 128 * k, T.qp, T.sp, 0, True, True).then_inc(S["t_f%d" % k], 1)
+    waits(P, "v_qz", "v_qe")
+    for h in range(4):
+        r = mm(T.pl, 128, T.qz, T.sz, 10 - 2 * (h % 2) - 8 * (h // 2), T.qp, T.sp, 64 * h, h == 0, h == 3)
+    r.then_inc(S.t_l, 1)
+    P.wait_ge(S.arr, arrivals)
+    for t in TO:
+        waits(P, "v_d%d" % t)
+        mm(pv[t], 128, T.qi, T.si, 128 * t, T.qx, T.sx, H if end else 0, True, True).then_inc(S["t_lv%d" % t], 1)
+    waits(P, "v_qw", "v_f0:4", "v_f1:4")
+    inner = (pf, [pv[0], pv[2]])
+    for i, (m0, m1, c) in enumerate(halves):
+        waits(P, "v_q" + c)
+        if i == 1:
+            waits(P, "s_lv0", "v_dl0", "s_lv2", "v_dl2")
+        for o in range(2):
+            mm(inner[i][o], 190, T.qw, T.sw, 128 * o, T.qm, T.sm, 8 * m0, True, False)
+            mm(inner[i][o], 190, T.qw, T.sw, 256 + 128 * o, T.qm, T.sm, 8 * m0 + 2, False, True).then_inc(S["t_o%s%d" % (c, o)], 1)
+    waits(P, "v_dc", "v_eq", "v_qme")
+    for o, pe in enumerate((T.pl, T.px)):
+        mm(pe, 128, T.qw, T.sw, 128 * o, T.qm, T.sm, 0, True, False)
+        mm(pe, 128, T.qw, T.sw, 256 + 128 * o, T.qm, T.sm, 2, False, True).then_inc(S["t_oe%d" % o], 1)
+
+    waits(C, "v_ones")
+    for i in range(2):
+        C.activation(T.zf[:, 1024 * i:1024 * i + 1024:2], T.one[:, 0:512], CP, 0.0, 0.0).then_inc(S.s_z, 1)
+    waits(C, "v_zt", "d_u:16")
+    for k in range(2):
+        for e in range(2):
+            C.activation(T.zt[:, 0:8, 10 + 4 * k + e, :], T.ub[:, k, :, :], CP).then_inc(S.s_zt, 1)
+    waits(C, "d_xe:32")
+    for h in range(4):
+        group(C.activation, 64 * h, 16, T.xe, EC[h] if EC[h] < H else EC[h] - (TC - 2 * H), CP).then_inc(S.s_xe, 1)
+    waits(C, "d_x:16")
+    for h in range(2):
+        group(C.activation, 64 * h + 16, 48, T.xt, IC[h], CP).then_inc(S.s_xi, 1)
+    for t in TO:
+        waits(C, "t_v%d" % t)
+        C.activation(vw[t % 2][:, t // 2:2 * TC:2], pv[t][:, 0:TC], CP).then_inc(S["s_v%d" % t], 1)
+    waits(C, "v_f0:4", "v_f1:4")
+    C.activation(T.zf[:, 515:2048:4], T.zf[:, 513:2048:4], CP).then_inc(S.s_fi, 1)
+    waits(C, "s_v1", "s_v3", "v_lv", "v_hz:%d" % hz, "v_d1", "v_d3")
+    for m0, m1, c in halves:
+        C.activation(T.gi[:, 32 * m0 + 1:32 * m1:2], T.v1[:, 0:vi].indirect(T.lv[:, m0:m1]), CP).then_inc(S["s_v" + c], 1)
+        waits(C, "v_ld")
+        C.activation(T.gi[:, 32 * m0:32 * m1:2], T.d1[:, 0:di].indirect(T.ld[:, m0:m1]), CP).then_inc(S["s_g" + c], 1)
+    C.activation(T.zf[:, 3:512:4], T.zf[:, 1:512:4], CP).then_inc(S.s_fe, 1)
+    waits(C, "s_v0", "s_v2", "v_d0", "v_d2")
+    for i in range(2):
+        C.activation(vw[i][:, 2 * DUP:WN], vw[i][:, 0:4 * H], CP).then_inc(S.s_vd, 1)
+        C.activation(dw[i][:, 2 * (DUP + PAD):WN + 2 * PAD], dw[i][:, 2 * PAD:2 * PAD + 4 * H], CP).then_inc(S.s_dd, 1)
+    ha, he = (TC + H, DUP) if last else (TC, TC + H if first else DUP)
+    for t in TO:
+        waits(C, "t_lv%d" % t)
+        C.activation(vw[t % 2][:, 2 * ha + t // 2:2 * he:2], pv[t][:, 0:he - ha], CP).then_inc(S["s_lv%d" % t], 1)
+    waits(C, "s_vd:2", "s_dd:2", "s_lv1", "s_lv3")
+    C.activation(T.gi[:, 1:512:2], T.v1[:].indirect(T.lv[:, 0:16]), CP).then_inc(S.s_vg, 1)
+    waits(C, "v_dl1", "v_dl3")
+    C.activation(T.gi[:, 0:512:2], T.d1[:].indirect(T.ld[:, 0:16]), CP).then_inc(S.s_ge, 1)
+    for i, (m0, m1, c) in enumerate(halves):
+        for o in range(2):
+            waits(C, "t_o%s%d" % (c, o))
+            for h in range(4):
+                a = TC * o + IC[h] + 24 * i
+                C.activation(T.ys[:, a:a + 24], inner[i][o][:, h % 2 + 4 * (h // 2):190:8], CP).then_inc(S.s_y, 1)
+    waits(C, "t_oe0")
+    edge_y(lambda a, b: C.activation(a, b, CP), 0, T.pl, S.s_ye)
+    waits(C, "v_y:4")
+    C.dma_start(T.y[:, 2 * TC - H:2 * TC], T.ys[:, 2 * TC - H:2 * TC]).then_inc(S.st2, 16)
+    waits(C, "st2:16")
+    waits(Y, "s_y:16")
+    for o in range(2):
+        Y.dma_start(T.y[:, TC * o + H:TC * o + TC - H], T.ys[:, TC * o + H:TC * o + TC - H]).then_inc(S.st1, 16)
+    waits(Y, "s_ye:4")
+    Y.dma_start(T.y[:, 0:H], T.ys[:, 0:H]).then_inc(S.st1, 16)
+    waits(Y, "v_y:4")
+    Y.dma_start(T.y[:, TC - H:TC + H], T.ys[:, TC - H:TC + H]).then_inc(S.st1, 16)
+    waits(Y, "st1:64")

@@ -1,31 +1,45 @@
 from concourse.bass import DstId, RemoteDMATransfer
 from concourse.mybir import dt, AluOpType, ActivationFunctionType
 
-H, TC, CL, PAD = 32, 256, 31, 8
-OWN, EP = 2 * H, TC
-EC = (16, 0, TC - 16, TC - 32)
-IC = (32, 80, 128, 176)
-DUP = TC + 2 * H
-WN = 2 * (DUP + 2 * H)
+H, TC, CL = 32, 256, 31
+ROT = 160
+EL = TC - ROT
+ROUND = 1.5 * 2.0 ** 23
+RUNS = {"a": (16, 32), "b": (0, 8), "e": (8, 16)}
+ORDER = {
+    "G": "part eye cols send w zeros vdup ddup add_a add_b",
+    "V": "fill bits m1 eye2 eye3 qe hs qx qz eye0 eye1 qu d2 d3 dl nl w eq end lv wz d0 ld d1 fr0 fr1 "
+         "p2a p3a p0a p1a p2b p3b p0b p1b qw h2 h3 h0 h1 hx p0e p1e scan2 scan3 qa m0e m1e qb qe2 ye1",
+    "T": "v2 v3 list v0 v1 f0 f1 h2 h3 h0 h1 oa ob oe",
+    "S": "zt u1 u2 m0 u3 tab1 u4 tab2 v2 tab3 v3 pick v0 v1 r0 r1 n0 n1 g2a g3a g0a g1a g2b g3b g0b g1b h2 h3 h0 h1 "
+         "g2e g3e e2 e3 ya0 ya1 yb0 yb1 ye0 se",
+    "Y": "sa0 sa1 sb0 sb1 se0 se1",
+}
 SCRATCH = {
     "ub": ("sbuf", [128, 2, 8, 4], "bfloat16"),
     "us": ("sbuf", [128, 2, 8, 16, 4], "bfloat16"),
     "zt": ("sbuf", [128, 9, 16, 4], "bfloat16"),
+    "vw": ("sbuf", [128, 4, 384], "float32"),
+    "dw": ("sbuf", [128, 4, 392], "float32"),
+    "zf": ("sbuf", [128, 1024], "float32"),
+    "gi": ("sbuf", [128, 2, 256], "float32"),
+    "pr": ("sbuf", [128, 512, 4], "float32"),
+    "mt": ("sbuf", [128, 4 * 514], "bfloat16"),
+    "ye": ("sbuf", [128, 4, 32], "float32"),
 }
-for names, width, kind in (("qp", 384, "q"), ("rq", H, "q"), ("qx", 320, "q"), ("qu", 256, "q"), ("qz", 144, "q"), ("qi qw qm", 512, "q"),
-                           ("sp", 384, "s"), ("rs", H, "s"), ("sx", 320, "s"), ("su", 256, "s"), ("sz", 144, "s"), ("si sw sm", 512, "s"),
-                           ("xe", 512, "b"), ("xp xt", 1024, "b"), ("one eye", 516, "b"), ("wb mt", 2048, "b"),
-                           ("pi b0 b1 b3", 1, "i"), ("nl", 64, "i"), ("fn", 512, "i"), ("z0 z1 hj hf hi he lim", 1, "f"), ("ic", 48, "f"),
-                           ("tab dc eq wl we wz", 64, "f"), ("lv ld", 64, "u"), ("zf gi", 2048, "f"), ("v0 v1", WN, "f"),
-                           ("d0 d1", WN + 2 * PAD, "f"), ("pr", 1024, "f"), ("ys", 512, "f"),
+for names, width, kind in (("rq", H, "q"), ("qx", 320, "q"), ("qu", 256, "q"), ("qz", 144, "q"), ("qi qw", 512, "q"), ("qm", 514, "q"),
+                           ("rs", H, "s"), ("sx", 320, "s"), ("su", 256, "s"), ("sz", 144, "s"), ("si sw", 512, "s"), ("sm", 514, "s"),
+                           ("xt", 1024, "b"), ("eye", 516, "b"), ("wb", 2048, "b"),
+                           ("pi b0 b1", 1, "i"), ("nl", 32, "i"), ("m0 m1 hs", 1, "f"),
+                           ("ic tab pa pb dl dc eq wl wz", 32, "f"), ("lv ld", 32, "u"), ("r1 fn ys", 512, "f"),
                            ("pf0 pf1 pl px pv0 pv1 pv2 pv3", 512, "p")):
     for name in names.split():
         SCRATCH[name] = ("psum" if kind == "p" else "sbuf", [128, width],
                          {"q": "float8_e4m3fn_x4", "s": "uint8", "b": "bfloat16", "i": "int32", "u": "uint16"}.get(kind, "float32"))
-SEMAPHORES = ("d_xe d_u d_x d_w st1 st2 ra rb arr loc g_p g_e g_c v_ones v_xp v_zt v_hz v_c1 v_c2 v_c3 v_c4 v_tab v_e v_qe v_u1 v_u2 v_u3 "
-              "v_qu v_qp v_qx v_qz v_xi v_n0 v_n1 v_f0 v_f1 v_dc v_eq v_nl v_wl v_we v_wz v_lv v_ld v_qw v_p v_sa v_sb v_ma v_mb v_qa v_qb "
-              "v_pe v_se v_me v_qme v_y s_z s_zt s_xe s_xi s_fi s_fe s_vd s_dd s_va s_vb s_ga s_gb s_vg s_ge s_y s_ye t_f0 t_f1 t_l t_oa0 "
-              "t_oa1 t_ob0 t_ob1 t_oe0 t_oe1").split() + [p + str(b) for p in ("s_v", "s_lv", "v_d", "v_dl", "t_v", "t_lv") for b in range(4)]
+SEMAPHORES = ("d_xe d_u d_x d_w d_ma d_mb st1 st2 ra rb arr loc g_p g_c g_e g_z g_vd g_dd v_eye v_zt v_hz v_b v_m1 v_hs v_qe v_qx v_qz v_qu "
+              "v_dl v_nl v_dc v_eq v_wl v_we v_wz v_lv v_ld v_f0 v_f1 v_pa v_pb v_pe v_qw v_qa v_qb v_qe2 v_dx v_se v_me v_y "
+              "s_zt s_u1 s_u2 s_u3 s_u4 s_m0 s_tab s_tb3 s_p s_r0 s_r1 s_n0 s_n1 s_va s_vb s_g2 s_g3 s_ya0 s_ya1 s_yb0 s_yb1 s_ye t_f0 t_f1 t_l "
+              "t_oa0 t_oa1 t_ob0 t_ob1 t_oe0 t_oe1").split() + [p + str(b) for p in ("v_e", "s_v", "s_h", "v_d", "v_h", "t_v", "t_h") for b in range(4)]
 
 
 def mask_of(engines):
@@ -42,8 +56,8 @@ def routes(T, topo, core):
         cand = [c for c in topo.cores_of(core) if c != core and topo.may_write(c, dst)]
         cand.sort(key=lambda c: (topo.die(c) != topo.die(core), c))
         relay = cand[side]
-        out.append((side, relay, dst, topo.engines(core, relay)[4 * side:4 * side + 4], topo.engines(relay, dst)[::2], EP + H * side,
-                    H if side == 1 or nb == 0 else 0))
+        out.append((side, relay, dst, topo.engines(core, relay)[4 * side:4 * side + 4], topo.engines(relay, dst)[::2], EL - H * side,
+                    TC + (H if side == 1 and nb < n - 1 else 0)))
     return out
 
 
@@ -71,255 +85,296 @@ def rank_program(g, core, T, topo):
     n = len(T.cores)
     first, last = rank == 0, rank == n - 1
     end = first or last
-    S, A, CP = T.sem, AluOpType, ActivationFunctionType.Copy
+    S, A, CP, ID = T.sem, AluOpType, ActivationFunctionType.Copy, ActivationFunctionType.Identity
     V, C, P, Y = g.vector, g.scalar, g.tensor, g.sync
-    pv = [T["pv%d" % b] for b in range(4)]
-    pf, vw, dw, TO = [T.pf0, T.pf1], [T.v0, T.v1], [T.d0, T.d1], (1, 3, 0, 2)
+    pv, pf = [T["pv%d" % b] for b in range(4)], [T.pf0, T.pf1]
+    banks = {"a": pf, "b": [T.pl, T.px], "e": [pv[0], pv[2]]}
+    hc = H if end else 2 * H
+    ring = TC + hc
+    wide = TC + H - 1 if first else ring + 2 * H - 1
+    again = [] if first else ["g_vd", "g_dd", "v_dx"]
+    own_v, own_d = ["s_v%d:2" % t for t in range(4)], ["v_d%d:2" % t for t in range(4)]
     out = routes(T, topo, core)
+    arrivals = sum(2 * len(q[4]) for nb in (rank - 1, rank + 1) if 0 <= nb < n for q in routes(T, topo, T.cores[nb]) if q[2] == core)
+    seen = {}
 
     def waits(q, *pairs):
         for name in pairs:
             a, _, c = name.partition(":")
-            q.wait_ge(S[a], int(c or 1))
+            if seen.get((q, a), 0) < int(c or 1):
+                seen[q, a] = int(c or 1)
+                {"G": g, "V": V, "S": C, "T": P, "Y": Y}[q].wait_ge(S[a], int(c or 1))
 
-    def group(call, to, cols, src, at, *more):
-        return call(T.xp[:, 4 * to:4 * (to + cols)], src[:, 4 * at:4 * (at + cols)], *more)
-    arrivals = sum(2 * len(q[4]) for nb in (rank - 1, rank + 1) if 0 <= nb < n for q in routes(T, topo, T.cores[nb]) if q[2] == core)
-    Y.dma_start(T.xe[:, 0:4 * H], T.x[:, 0:4 * H]).then_inc(S.d_xe, 16)
-    C.dma_start(T.xe[:, 4 * H:8 * H], T.x[:, 4 * (TC - H):4 * TC]).then_inc(S.d_xe, 16)
-    Y.dma_start(T.ub[:], T.u[:, 0:64]).then_inc(S.d_u, 16)
-    Y.dma_start(T.xt[:], T.x[:]).then_inc(S.d_x, 16)
-    Y.wait_ge(S.d_x, 16)
-    Y.dma_start(T.wb[:], T.w[:]).then_inc(S.d_w, 16)
-    g.iota(T.pi[:], [[0, 1]], 0, 1).then_inc(S.g_p, 1)
-    g.wait_ge(S.v_ones, 1)
-    g.affine_select(T.eye[:], T.one[:], [[-1, 516]], A.is_equal, 0.0, 4, 4).then_inc(S.g_e, 1)
-    g.iota(T.ic[:], [[1, 48]], 0, 0, allow_small_or_imprecise_dtypes=True).then_inc(S.g_c, 1)
-    g.wait_ge(S.v_qe, 1)
-    codes, planes = [], []
-    for side, relay, dst, near, far, col, land in out:
-        rid, pid = topo.addr(relay, core)
-        to = [DstId(rid=rid, pnc=pid)]
-        codes.append(RemoteDMATransfer(dst_ids=to, dma_engine_mask=mask_of(near), remote_sem=S.ra,
-                                       src=T.qp[:, col:col + H].bitcast(dt.uint8), dst=T.rq[:, 0:H].bitcast(dt.uint8)))
-        planes.append(RemoteDMATransfer(dst_ids=to, dma_engine_mask=mask_of(near), remote_sem=S.rb,
-                                        src=T.sp[:, col:col + H], dst=T.rs[:, 0:H]))
-    g.remote_dma_fused(codes, local_sem=S.loc)
-    g.remote_dma_fused(planes, local_sem=S.loc)
-    g.wait_ge(S.loc, sum(2 * len(q[3]) for q in out))
-    V.memset(T.one[:], 1.0).then_inc(S.v_ones, 1)
-    V.memset(T.xe[:, 8 * H:512], 0.0).then_inc(S.v_xp, 1)
-    V.memset(T.zt[:], 0.0).then_inc(S.v_zt, 1)
-    hz = 6 if end else 2
-    for i in range(2):
-        V.memset(dw[i][:, 0:2 * PAD], 0.0).then_inc(S.v_hz, 1)
-        if end:
-            a, e = (TC + H - 1, DUP) if first else (TC - 1, TC + H)
-            V.memset(vw[i][:, 2 * a + 2:2 * e], 0.0).then_inc(S.v_hz, 1)
-            V.memset(dw[i][:, 2 * (a + PAD):2 * (e + PAD)], 0.0).then_inc(S.v_hz, 1)
-    waits(V, "g_p")
-    for b, bit in ((T.b0, 1), (T.b1, 2), (T.b3, 8)):
-        V.tensor_scalar(b[:], T.pi[:], bit, None, A.bitwise_and).then_inc(S.v_c1, 1)
-    waits(V, "v_c1:3")
-    V.tensor_scalar(T.z0[:], T.b0[:], 0.5, float(PAD), A.mult, A.add).then_inc(S.v_c2, 1)
-    V.tensor_scalar(T.z1[:], T.b0[:], 0.5, float(PAD + TC - 1 + 1000), A.mult, A.add).then_inc(S.v_c2, 1)
-    waits(V, "v_c2:2")
-    V.tensor_scalar(T.hj[:], T.b1[:], 24.0, T.z0[:], A.mult, A.add).then_inc(S.v_c3, 1)
-    V.tensor_scalar(T.hf[:], T.b1[:], -8.0, T.z0[:], A.mult, A.add).then_inc(S.v_c3, 1)
-    V.tensor_scalar(T.lim[:], T.b3[:], -125.0, T.z1[:], A.mult, A.add).then_inc(S.v_c4, 1)
-    waits(V, "v_c3:2")
-    V.tensor_scalar(T.hi[:], T.b3[:], 12.0, T.hj[:], A.mult, A.add).then_inc(S.v_c4, 1)
-    V.tensor_scalar(T.he[:], T.b3[:], 28.0 if first else -12.0, T.hf[:], A.mult, A.add).then_inc(S.v_c4, 1)
+    def words(r):
+        return slice(16 * RUNS[r][0], 16 * RUNS[r][1])
 
-    def eyes(bs):
-        for b in bs:
-            V.quantize_mx(T.qi[:, 128 * b:128 * b + 128], T.si[:, 128 * b:128 * b + 128], T.eye[:, 4 - b:516 - b]).then_inc(S.v_e, 1)
-    waits(V, "g_e")
-    eyes((1, 3))
-    waits(V, "v_xp", "d_xe:32")
-    V.quantize_mx(T.qp[:, EP:EP + 128], T.sp[:, EP:EP + 128], T.xe[:]).then_inc(S.v_qe, 1)
-    waits(V, "d_u:16")
-    for q in range(4):
-        V.tensor_copy(T.us[:, :, :, q, :], T.ub[:]).then_inc(S.v_u1, 1)
-    eyes((0,))
-    waits(V, "v_u1:4")
-    V.tensor_copy(T.us[:, :, :, 4:8, :], T.us[:, :, :, 0:4, :]).then_inc(S.v_u2, 1)
-    eyes((2,))
-    waits(V, "v_u2")
-    V.tensor_copy(T.us[:, :, :, 8:16, :], T.us[:, :, :, 0:8, :]).then_inc(S.v_u3, 1)
-    waits(V, "d_x:16")
-    V.quantize_mx(T.qx[:, OWN:OWN + TC], T.sx[:, OWN:OWN + TC], T.xt[:]).then_inc(S.v_qx, 1)
-    for h in (2, 3):
-        group(V.tensor_copy, 64 * h + 16, 48, T.xt, IC[h]).then_inc(S.v_xi, 1)
-    waits(V, "v_u3")
-    V.quantize_mx(T.qu[:], T.su[:], T.us[:]).then_inc(S.v_qu, 1)
-    waits(V, "v_xi:2", "s_xe:4", "s_xi:2")
-    V.quantize_mx(T.qp[:, 0:TC], T.sp[:, 0:TC], T.xp[:]).then_inc(S.v_qp, 1)
-    waits(V, "s_zt:4")
-    V.quantize_mx(T.qz[:], T.sz[:], T.zt[:]).then_inc(S.v_qz, 1)
-    waits(V, "v_c4:3", "g_c")
-    V.tensor_scalar(T.tab[:, 0:16], T.ic[:, 0:16], T.he[:], float(EC[0] + (0 if first else DUP)), A.add, A.add).then_inc(S.v_tab, 1)
-    V.tensor_scalar(T.tab[:, 16:64], T.ic[:], T.hi[:], float(IC[0]), A.add, A.add).then_inc(S.v_tab, 1)
+    def m_of(r, t=0, every=1):
+        return T.mt[:, 8 + 64 * RUNS[r][0] + t:8 + 64 * RUNS[r][1]:every]
 
-    def own_d(t):
-        waits(V, "s_v%d" % t)
-        V.tensor_tensor(dw[t % 2][:, 2 * PAD + t // 2:2 * (PAD + TC - 1):2], pv[t][:, 1:TC],
-                        vw[t % 2][:, t // 2:2 * (TC - 1):2], A.subtract).then_inc(S["v_d%d" % t], 1)
+    def fr_of(r):
+        return T.zf[:, 32 * RUNS[r][0] + 1:32 * RUNS[r][1]:2]
 
-    def fr(k):
-        waits(V, "v_n%d" % k)
-        for h in range(4):
-            q = 4 * k + 2 * (h % 2) + 8 * (h // 2)
-            a = 256 * k + 64 * h
-            V.tensor_tensor(T.zf[:, 2 * q + 1:2048:32], pf[k][:, 64 * h:64 * h + 64], T.fn[:, a:a + 64],
-                            A.subtract).then_inc(S["v_f%d" % k], 1)
-    own_d(1)
-    own_d(3)
-    for k in range(2):
-        waits(V, "t_f%d" % k)
-        V.tensor_scalar(T.fn[:, TC * k:TC * k + TC], pf[k][:, 0:TC], -float(CL), float(CL), A.max, A.min).then_inc(S["v_n%d" % k], 1)
-    fr(0)
-    waits(V, "t_l")
-    V.tensor_scalar(T.dc[:], T.pl[:, 0:64], -float(CL), float(CL), A.max, A.min).then_inc(S.v_dc, 1)
-    fr(1)
-    waits(V, "v_dc")
-    V.tensor_copy(T.nl[:], T.dc[:]).then_inc(S.v_nl, 1)
-    V.tensor_tensor(T.eq[:], T.dc[:], T.pl[:, 0:64], A.is_equal).then_inc(S.v_eq, 1)
-    waits(V, "v_tab:2", "v_nl")
-    V.tensor_tensor(T.wl[:], T.nl[:], T.tab[:], A.add).then_inc(S.v_wl, 1)
-    own_d(0)
-    waits(V, "v_wl", "v_eq")
-    wl = T.wl
-    if end:
-        wl = T.we
-        V.tensor_scalar(T.we[:], T.wl[:], T.z0[:] if first else T.lim[:], None, A.max if first else A.min).then_inc(S.v_we, 1)
-        waits(V, "v_we")
-    V.tensor_tensor(T.wz[:], wl[:], T.eq[:], A.mult).then_inc(S.v_wz, 1)
-    V.tensor_scalar(T.lv[:], wl[:], 2.0, -2.0 * PAD, A.mult, A.add).then_inc(S.v_lv, 1)
-    own_d(2)
-    waits(V, "v_wz")
-    V.tensor_scalar(T.ld[:], T.wz[:], 2.0, None, A.mult).then_inc(S.v_ld, 1)
-    di, vi = 2 * (PAD + TC - 1), 2 * (TC - 1)
-    waits(V, "v_ld", "v_lv", "s_fi", "v_hz:%d" % hz, "v_d0", "v_d2")
-    V.tensor_tensor(T.pr[:, 256:1024], T.d0[:, 0:di].indirect(T.ld[:, 16:64]), T.zf[:, 513:2048:2], A.mult).then_inc(S.v_p, 1)
-    waits(V, "d_w:16")
-    V.quantize_mx(T.qw[:], T.sw[:], T.wb[:]).then_inc(S.v_qw, 1)
-    waits(V, "s_z:2")
-    halves = ((16, 40, "a"), (40, 64, "b"))
-    for m0, m1, c in halves:
-        waits(V, "s_v" + c, "s_g" + c)
-        V.tensor_tensor_scan(T.mt[:, 32 * m0:32 * m1], T.zf[:, 32 * m0:32 * m1], T.gi[:, 32 * m0:32 * m1], 0.0,
-                             A.mult, A.add).then_inc(S["v_s" + c], 1)
-    waits(V, "v_p")
-    for m0, m1, c in halves:
-        waits(V, "v_s" + c)
-        V.tensor_tensor(T.mt[:, 32 * m0:32 * m1:2], T.v0[:, 0:vi].indirect(T.lv[:, m0:m1]), T.pr[:, 16 * m0:16 * m1],
-                        A.add).then_inc(S["v_m" + c], 1)
-    for m0, m1, c in halves:
-        waits(V, "v_m" + c)
-        V.quantize_mx(T.qm[:, 8 * m0:8 * m1], T.sm[:, 8 * m0:8 * m1], T.mt[:, 32 * m0:32 * m1]).then_inc(S["v_q" + c], 1)
-    a, e, b = (TC + H, DUP, 1) if last else (TC - 1, TC + H - 1 if first else DUP, 0)
-    for t in TO:
-        waits(V, "s_lv%d" % t)
-        V.tensor_tensor(dw[t % 2][:, 2 * (PAD + a) + t // 2:2 * (PAD + e):2], pv[t][:, b:b + e - a],
-                        vw[t % 2][:, 2 * a + t // 2:2 * e:2], A.subtract).then_inc(S["v_dl%d" % t], 1)
-    waits(V, "s_dd:2", "s_vd:2", "s_fe", "v_dl0", "v_dl2")
-    V.tensor_tensor(T.pr[:, 0:256], T.d0[:].indirect(T.ld[:, 0:16]), T.zf[:, 1:512:2], A.mult).then_inc(S.v_pe, 1)
-    waits(V, "s_vg", "s_ge")
-    V.tensor_tensor_scan(T.mt[:, 0:512], T.zf[:, 0:512], T.gi[:, 0:512], 0.0, A.mult, A.add).then_inc(S.v_se, 1)
-    waits(V, "v_pe", "v_se")
-    V.tensor_tensor(T.mt[:, 0:512:2], T.v0[:].indirect(T.lv[:, 0:16]), T.pr[:, 0:256], A.add).then_inc(S.v_me, 1)
-    waits(V, "v_me")
-    V.quantize_mx(T.qm[:, 0:128], T.sm[:, 0:128], T.mt[:, 0:512]).then_inc(S.v_qme, 1)
+    def v_at(t, r):
+        return T.vw[:, t, 0:wide if r == "e" else TC - 1].indirect(T.lv[:, RUNS[r][0]:RUNS[r][1]])
 
-    def edge_y(call, o, src, sem):
-        for h in range(4):
-            call(T.ys[:, TC * o + EC[h]:TC * o + EC[h] + 16], src[:, h % 2 + 4 * (h // 2):128:8]).then_inc(sem, 1)
-    waits(V, "t_oe1")
-    edge_y(V.tensor_copy, 1, T.px, S.v_y)
+    def d_at(t, r):
+        return T.dw[:, t, 0:1 + (wide if r == "e" else TC - 1)].indirect(T.ld[:, RUNS[r][0]:RUNS[r][1]])
+
+    def zeros(ap, count):
+        return g.iota(ap, [[0, count]], 0, 0, allow_small_or_imprecise_dtypes=True)
+
+    def gpsimd(step):
+        if step == "part":
+            g.iota(T.pi[:], [[0, 1]], 0, 1).then_inc(S.g_p, 1)
+        elif step == "eye":
+            waits("G", "v_eye")
+            g.affine_select(T.eye[:, 0:516:4], T.eye[:, 0:516:4], [[-1, 129]], A.not_equal, 1.0, 1, 1).then_inc(S.g_e, 1)
+        elif step == "cols":
+            g.iota(T.ic[:], [[8, 32]], 1, 0, allow_small_or_imprecise_dtypes=True).then_inc(S.g_c, 1)
+        elif step == "send":
+            waits("G", "v_qe")
+            codes, planes = [], []
+            for side, relay, dst, near, far, col, land in out:
+                rid, pid = topo.addr(relay, core)
+                to = [DstId(rid=rid, pnc=pid)]
+                codes.append(RemoteDMATransfer(dst_ids=to, dma_engine_mask=mask_of(near), remote_sem=S.ra,
+                                               src=T.qx[:, col:col + H].bitcast(dt.uint8), dst=T.rq[:, 0:H].bitcast(dt.uint8)))
+                planes.append(RemoteDMATransfer(dst_ids=to, dma_engine_mask=mask_of(near), remote_sem=S.rb,
+                                                src=T.sx[:, col:col + H], dst=T.rs[:, 0:H]))
+            g.remote_dma_fused(codes, local_sem=S.loc)
+            g.remote_dma_fused(planes, local_sem=S.loc)
+        elif step == "w":
+            waits("G", "d_x:16")
+            g.dma_start(T.wb[:], T.w[:]).then_inc(S.d_w, 16)
+        elif step == "zeros":
+            zeros(T.mt[:, 0:8], 8).then_inc(S.g_z, 1)
+            zeros(T.zf[:, 32 * RUNS["e"][0]:32 * RUNS["e"][1]:2], 128).then_inc(S.g_z, 1)
+        elif step == "vdup" and not first:
+            waits("G", *own_v)
+            g.affine_select(T.vw[:, :, ring:ring + 2 * H], T.vw[:, :, 0:2 * H], [[0, 8 * H]], A.is_equal, 0.0, 0, 0).then_inc(S.g_vd, 1)
+        elif step == "ddup" and not first:
+            waits("G", *own_d)
+            g.affine_select(T.dw[:, :, 1 + ring:1 + ring + 2 * H], T.dw[:, :, 1:1 + 2 * H], [[0, 8 * H]], A.is_equal, 0.0, 0, 0).then_inc(S.g_dd, 1)
+        elif step[:3] == "add":
+            r = step[4]
+            waits("G", "v_p%s:4" % r, "s_v%s:4" % r)
+            g.dma_start(m_of(r), T.pr[:, words(r), :], accum_op=A.add).then_inc(S["d_m" + r], 16)
+
+    def vector(step):
+        t = int(step[-1]) if step[-1].isdigit() else int(step[1]) if step[1:2].isdigit() else None
+        if step == "fill":
+            V.memset(T.eye[:], 0.0).then_inc(S.v_eye, 1)
+            V.memset(T.zt[:], 0.0).then_inc(S.v_zt, 1)
+            V.memset(T.dw[:, :, 0:TC + 1:TC] if last else T.dw[:, :, 0], 0.0).then_inc(S.v_hz, 1)
+        elif step == "bits":
+            waits("V", "g_p")
+            V.tensor_scalar(T.b0[:], T.pi[:], 1, None, A.bitwise_and).then_inc(S.v_b, 1)
+            V.tensor_scalar(T.b1[:], T.pi[:], 1, 6, A.logical_shift_right, A.bitwise_and).then_inc(S.v_b, 1)
+        elif step == "m1":
+            waits("V", "v_b:2")
+            V.tensor_copy(T.m1[:], T.b0[:]).then_inc(S.v_m1, 1)
+        elif step == "hs":
+            waits("V", "v_m1")
+            V.tensor_scalar(T.hs[:], T.b1[:], T.m1[:], None, A.add).then_inc(S.v_hs, 1)
+        elif step[:3] == "eye":
+            waits("V", "g_e")
+            V.quantize_mx(T.qi[:, 128 * t:128 * t + 128], T.si[:, 128 * t:128 * t + 128], T.eye[:, 4 - t:516 - t]).then_inc(S["v_e%d" % t], 1)
+        elif step == "qe":
+            waits("V", "d_xe:32")
+            V.quantize_mx(T.qx[:, 0:128], T.sx[:, 0:128], T.xt[:, 0:512]).then_inc(S.v_qe, 1)
+        elif step == "qx":
+            waits("V", "d_x:16")
+            V.quantize_mx(T.qx[:, 128:256], T.sx[:, 128:256], T.xt[:, 512:1024]).then_inc(S.v_qx, 1)
+        elif step == "qz":
+            waits("V", "s_zt:4")
+            V.quantize_mx(T.qz[:], T.sz[:], T.zt[:]).then_inc(S.v_qz, 1)
+        elif step == "qu":
+            waits("V", "s_u4")
+            V.quantize_mx(T.qu[:], T.su[:], T.us[:]).then_inc(S.v_qu, 1)
+        elif step == "qw":
+            waits("V", "d_w:16")
+            V.quantize_mx(T.qw[:], T.sw[:], T.wb[:]).then_inc(S.v_qw, 1)
+        elif step == "dl":
+            waits("V", "s_p:2")
+            V.tensor_tensor(T.dl[:], T.pa[:], T.pb[:], A.add).then_inc(S.v_dl, 1)
+        elif step == "nl":
+            waits("V", "v_dl")
+            V.tensor_scalar(T.nl[:], T.dl[:], -float(CL), float(CL), A.max, A.min).then_inc(S.v_nl, 1)
+            V.tensor_scalar(T.dc[:], T.dl[:], -float(CL), float(CL), A.max, A.min).then_inc(S.v_dc, 1)
+        elif step == "w":
+            waits("V", "v_nl", "s_tb3")
+            V.tensor_tensor(T.wl[:], T.nl[:], T.tab[:], A.add).then_inc(S.v_wl, 1)
+        elif step == "eq":
+            waits("V", "v_dc")
+            V.tensor_tensor(T.eq[:], T.dc[:], T.dl[:], A.is_equal).then_inc(S.v_eq, 1)
+        elif step == "end":
+            if end:
+                waits("V", "v_wl")
+                wl = T.wl[:, 8:12] if last else T.wl[:]
+                V.tensor_scalar(wl, wl, float(TC) if last else 1.0, None, A.min if last else A.max).then_inc(S.v_we, 1)
+        elif step == "lv":
+            waits("V", "v_we" if end else "v_wl")
+            V.tensor_scalar(T.lv[:], T.wl[:], -1.0, None, A.add).then_inc(S.v_lv, 1)
+        elif step == "wz":
+            waits("V", "v_we" if end else "v_wl", "v_eq")
+            V.tensor_tensor(T.wz[:], T.wl[:], T.eq[:], A.mult).then_inc(S.v_wz, 1)
+        elif step == "ld":
+            waits("V", "v_wz")
+            V.tensor_copy(T.ld[:], T.wz[:]).then_inc(S.v_ld, 1)
+        elif step[0] == "d":
+            waits("V", own_v[t])
+            V.tensor_tensor(T.dw[:, t, 1:ROT], pv[t][:, EL + 1:TC], T.vw[:, t, 0:ROT - 1], A.subtract).then_inc(S["v_d%d" % t], 1)
+            V.tensor_tensor(T.dw[:, t, ROT:TC], pv[t][:, 0:EL], T.vw[:, t, ROT - 1:TC - 1], A.subtract).then_inc(S["v_d%d" % t], 1)
+        elif step[:2] == "fr":
+            waits("V", "s_n%d" % t)
+            for h in range(2):
+                V.tensor_tensor(T.zf[:, 4 * t + 2 * h + 1:1024:8], pf[t][:, h:TC:2], T.fn[:, TC * t + h:TC * t + TC:2],
+                                A.subtract).then_inc(S["v_f%d" % t], 1)
+        elif step[0] == "p":
+            r = step[2]
+            waits("V", "v_ld", "v_hz", "v_f0:2", "v_f1:2", own_d[t], *(["v_h%d" % t] + again if r == "e" else []))
+            V.tensor_tensor(T.pr[:, words(r), t], d_at(t, r), fr_of(r), A.mult).then_inc(S["v_p" + r], 1)
+        elif step == "hx":
+            if not first:
+                waits("V", "s_h0", "s_h1", "s_h2", "s_h3")
+                V.tensor_tensor(T.dw[:, :, ring], T.vw[:, :, 0], T.vw[:, :, ring - 1], A.subtract).then_inc(S.v_dx, 1)
+        elif step[0] == "h":
+            a = TC if last else TC - 1
+            waits("V", "s_h%d" % t)
+            V.tensor_tensor(T.dw[:, t, 1 + a:ring], pv[t][:, 128 - (ring - 1 - a):128], T.vw[:, t, a:ring - 1], A.subtract).then_inc(S["v_h%d" % t], 1)
+        elif step[:4] == "scan":
+            waits("V", "g_z:2", "s_g%d:2" % t)
+            V.tensor_tensor_scan(m_of("e", t - 2, 2), T.zf[:, 32 * RUNS["e"][0]:32 * RUNS["e"][1]], T.gi[:, t - 2], 0.0,
+                                 A.mult, A.add).then_inc(S.v_se, 1)
+        elif step[0] == "m":
+            waits("V", "v_pe:2", "v_se:2")
+            V.tensor_tensor(m_of("e", t, 4), v_at(t, "e"), T.pr[:, words("e"), t], A.add).then_inc(S.v_me, 1)
+        elif step[0] == "q":
+            r = step[1]
+            waits("V", *{"a": ["d_ma:16"], "b": ["d_mb:16", "g_z:2"], "e": ["v_me:2"]}[r])
+            a, e = (0 if r == "b" else 2 + 16 * RUNS[r][0]), 2 + 16 * RUNS[r][1]
+            V.quantize_mx(T.qm[:, a:e], T.sm[:, a:e], T.mt[:, 4 * a:4 * e]).then_inc(S["v_" + step], 1)
+        elif step == "ye1":
+            waits("V", "t_oe1")
+            for h in range(2):
+                V.tensor_copy(T.ye[:, 2:4, h:32:2], pv[2][:, h:128:4]).then_inc(S.v_y, 1)
 
     def mm(o, cols, lq, ls, a, rq, rs, c, start, stop):
         return P.matmul_mx(o[:, 0:cols], lq[:, a:a + 128], ls[:, a:a + 128], rq[:, c:c + cols], rs[:, c:c + cols], start, stop)
-    waits(P, "v_e:4", "v_qx")
-    for t in TO:
-        mm(pv[t], TC, T.qi, T.si, 128 * t, T.qx, T.sx, OWN, True, True).then_inc(S["t_v%d" % t], 1)
-    waits(P, "v_qu", "v_qp")
-    for k in range(2):
-        mm(pf[k], TC, T.qu, T.su, 128 * k, T.qp, T.sp, 0, True, True).then_inc(S["t_f%d" % k], 1)
-    waits(P, "v_qz", "v_qe")
-    for h in range(4):
-        r = mm(T.pl, 128, T.qz, T.sz, 10 - 2 * (h % 2) - 8 * (h // 2), T.qp, T.sp, 64 * h, h == 0, h == 3)
-    r.then_inc(S.t_l, 1)
-    P.wait_ge(S.arr, arrivals)
-    for t in TO:
-        waits(P, "v_d%d" % t)
-        mm(pv[t], 128, T.qi, T.si, 128 * t, T.qx, T.sx, H if end else 0, True, True).then_inc(S["t_lv%d" % t], 1)
-    waits(P, "v_qw", "v_f0:4", "v_f1:4")
-    inner = (pf, [pv[0], pv[2]])
-    for i, (m0, m1, c) in enumerate(halves):
-        waits(P, "v_q" + c)
-        if i == 1:
-            waits(P, "s_lv0", "v_dl0", "s_lv2", "v_dl2")
-        for o in range(2):
-            mm(inner[i][o], 190, T.qw, T.sw, 128 * o, T.qm, T.sm, 8 * m0, True, False)
-            mm(inner[i][o], 190, T.qw, T.sw, 256 + 128 * o, T.qm, T.sm, 8 * m0 + 2, False, True).then_inc(S["t_o%s%d" % (c, o)], 1)
-    waits(P, "v_dc", "v_eq", "v_qme")
-    for o, pe in enumerate((T.pl, T.px)):
-        mm(pe, 128, T.qw, T.sw, 128 * o, T.qm, T.sm, 0, True, False)
-        mm(pe, 128, T.qw, T.sw, 256 + 128 * o, T.qm, T.sm, 2, False, True).then_inc(S["t_oe%d" % o], 1)
 
-    waits(C, "v_ones")
-    for i in range(2):
-        C.activation(T.zf[:, 1024 * i:1024 * i + 1024:2], T.one[:, 0:512], CP, 0.0, 0.0).then_inc(S.s_z, 1)
-    waits(C, "v_zt", "d_u:16")
-    for k in range(2):
-        for e in range(2):
-            C.activation(T.zt[:, 0:8, 10 + 4 * k + e, :], T.ub[:, k, :, :], CP).then_inc(S.s_zt, 1)
-    waits(C, "d_xe:32")
-    for h in range(4):
-        group(C.activation, 64 * h, 16, T.xe, EC[h] if EC[h] < H else EC[h] - (TC - 2 * H), CP).then_inc(S.s_xe, 1)
-    waits(C, "d_x:16")
-    for h in range(2):
-        group(C.activation, 64 * h + 16, 48, T.xt, IC[h], CP).then_inc(S.s_xi, 1)
-    for t in TO:
-        waits(C, "t_v%d" % t)
-        C.activation(vw[t % 2][:, t // 2:2 * TC:2], pv[t][:, 0:TC], CP).then_inc(S["s_v%d" % t], 1)
-    waits(C, "v_f0:4", "v_f1:4")
-    C.activation(T.zf[:, 515:2048:4], T.zf[:, 513:2048:4], CP).then_inc(S.s_fi, 1)
-    waits(C, "s_v1", "s_v3", "v_lv", "v_hz:%d" % hz, "v_d1", "v_d3")
-    for m0, m1, c in halves:
-        C.activation(T.gi[:, 32 * m0 + 1:32 * m1:2], T.v1[:, 0:vi].indirect(T.lv[:, m0:m1]), CP).then_inc(S["s_v" + c], 1)
-        waits(C, "v_ld")
-        C.activation(T.gi[:, 32 * m0:32 * m1:2], T.d1[:, 0:di].indirect(T.ld[:, m0:m1]), CP).then_inc(S["s_g" + c], 1)
-    C.activation(T.zf[:, 3:512:4], T.zf[:, 1:512:4], CP).then_inc(S.s_fe, 1)
-    waits(C, "s_v0", "s_v2", "v_d0", "v_d2")
-    for i in range(2):
-        C.activation(vw[i][:, 2 * DUP:WN], vw[i][:, 0:4 * H], CP).then_inc(S.s_vd, 1)
-        C.activation(dw[i][:, 2 * (DUP + PAD):WN + 2 * PAD], dw[i][:, 2 * PAD:2 * PAD + 4 * H], CP).then_inc(S.s_dd, 1)
-    ha, he = (TC + H, DUP) if last else (TC, TC + H if first else DUP)
-    for t in TO:
-        waits(C, "t_lv%d" % t)
-        C.activation(vw[t % 2][:, 2 * ha + t // 2:2 * he:2], pv[t][:, 0:he - ha], CP).then_inc(S["s_lv%d" % t], 1)
-    waits(C, "s_vd:2", "s_dd:2", "s_lv1", "s_lv3")
-    C.activation(T.gi[:, 1:512:2], T.v1[:].indirect(T.lv[:, 0:16]), CP).then_inc(S.s_vg, 1)
-    waits(C, "v_dl1", "v_dl3")
-    C.activation(T.gi[:, 0:512:2], T.d1[:].indirect(T.ld[:, 0:16]), CP).then_inc(S.s_ge, 1)
-    for i, (m0, m1, c) in enumerate(halves):
-        for o in range(2):
-            waits(C, "t_o%s%d" % (c, o))
+    def tensor(step):
+        t = int(step[1]) if step[1].isdigit() else None
+        if step[0] == "v":
+            waits("T", "v_qe", "v_qx", "v_e%d" % t)
+            mm(pv[t], TC, T.qi, T.si, 128 * t, T.qx, T.sx, 0, True, True).then_inc(S["t_v%d" % t], 1)
+        elif step == "list":
+            waits("T", "v_qz")
             for h in range(4):
-                a = TC * o + IC[h] + 24 * i
-                C.activation(T.ys[:, a:a + 24], inner[i][o][:, h % 2 + 4 * (h // 2):190:8], CP).then_inc(S.s_y, 1)
-    waits(C, "t_oe0")
-    edge_y(lambda a, b: C.activation(a, b, CP), 0, T.pl, S.s_ye)
-    waits(C, "v_y:4")
-    C.dma_start(T.y[:, 2 * TC - H:2 * TC], T.ys[:, 2 * TC - H:2 * TC]).then_inc(S.st2, 16)
-    waits(C, "st2:16")
-    waits(Y, "s_y:16")
-    for o in range(2):
-        Y.dma_start(T.y[:, TC * o + H:TC * o + TC - H], T.ys[:, TC * o + H:TC * o + TC - H]).then_inc(S.st1, 16)
-    waits(Y, "s_ye:4")
-    Y.dma_start(T.y[:, 0:H], T.ys[:, 0:H]).then_inc(S.st1, 16)
-    waits(Y, "v_y:4")
-    Y.dma_start(T.y[:, TC - H:TC + H], T.ys[:, TC - H:TC + H]).then_inc(S.st1, 16)
-    waits(Y, "st1:64")
+                r = mm(T.pl, TC - 6, T.qz, T.sz, 12 - 4 * h, T.qx, T.sx, 2 * h, h == 0, h == 3)
+            r.then_inc(S.t_l, 1)
+        elif step[0] == "f":
+            waits("T", "v_qu")
+            mm(pf[t], TC, T.qu, T.su, 128 * t, T.qx, T.sx, 0, True, True).then_inc(S["t_f%d" % t], 1)
+        elif step[0] == "h":
+            waits("T", "arr:%d" % arrivals, own_d[t])
+            mm(pv[t], 128, T.qi, T.si, 128 * t, T.qx, T.sx, ring - 128, True, True).then_inc(S["t_h%d" % t], 1)
+        else:
+            r = step[1]
+            waits("T", "v_qw", "v_f0:2", "v_f1:2", "s_p:2", *{"a": ["v_qa"], "b": ["v_qb"], "e": ["v_qa", "v_qe2"]}[r])
+            a, cols = {"a": (2 + 16 * RUNS[r][0], 254), "b": (0, 128), "e": (2 + 16 * RUNS[r][0], 128)}[r]
+            for o in range(2):
+                mm(banks[r][o], cols, T.qw, T.sw, 128 * o, T.qm, T.sm, a, True, False)
+                mm(banks[r][o], cols, T.qw, T.sw, 256 + 128 * o, T.qm, T.sm, a + 2, False, True).then_inc(S["t_o%s%d" % (r, o)], 1)
+
+    own_y = {"a": (0, 254, H, ROT), "b": (2, 128, ROT, TC - H)}
+
+    def scalar(step):
+        t = int(step[-1]) if step[-1].isdigit() else int(step[1]) if step[1:2].isdigit() else None
+        if step == "zt":
+            waits("S", "v_zt", "d_u:16")
+            for k in range(2):
+                for e in range(2):
+                    C.activation(T.zt[:, 0:8, 12 + 2 * k + e, :], T.ub[:, k, :, :], CP).then_inc(S.s_zt, 1)
+        elif step == "u1":
+            waits("S", "d_u:16")
+            for q in range(2):
+                C.activation(T.us[:, :, :, q, :], T.ub[:], CP).then_inc(S.s_u1, 1)
+        elif step[0] == "u":
+            waits("S", "s_u1:2", "s_u%d" % (t - 1))
+            c = 2 ** (t - 1)
+            C.activation(T.us[:, :, :, c:2 * c, :], T.us[:, :, :, 0:c, :], CP).then_inc(S["s_u%d" % t], 1)
+        elif step == "m0":
+            waits("S", "v_m1")
+            C.activation(T.m0[:], T.m1[:], CP, 1.0, -1.0).then_inc(S.s_m0, 1)
+        elif step == "tab1":
+            waits("S", "v_hs", "g_c")
+            C.activation(T.tab[:, 0:12], T.ic[:, 20:32], ID, T.hs[:]).then_inc(S.s_tab, 1)
+        elif step == "tab2":
+            waits("S", "v_hs", "g_c")
+            C.activation(T.tab[:, 12:32], T.ic[:, 0:20], ID, T.hs[:]).then_inc(S.s_tab, 1)
+        elif step == "tab3":
+            waits("S", "s_tab:2")
+            C.activation(T.tab[:, 12:16], T.tab[:, 12:16], CP, 0.0 if first else float(ring)).then_inc(S.s_tb3, 1)
+        elif step[0] == "v":
+            waits("S", "t_v%d" % t)
+            C.activation(T.vw[:, t, 0:ROT], pv[t][:, EL:TC], CP).then_inc(S["s_v%d" % t], 1)
+            C.activation(T.vw[:, t, ROT:TC], pv[t][:, 0:EL], CP).then_inc(S["s_v%d" % t], 1)
+        elif step == "pick":
+            waits("S", "t_l", "s_m0")
+            C.activation(T.pa[:], T.pl[:, 0:TC - 6:8], CP, 0.0, T.m0[:]).then_inc(S.s_p, 1)
+            C.activation(T.pb[:], T.pl[:, 1:TC - 6:8], CP, 0.0, T.m1[:]).then_inc(S.s_p, 1)
+        elif step[0] == "r":
+            waits("S", "t_f%d" % t)
+            C.activation(T.r1[:, TC * t:TC * t + TC], pf[t][:, 0:TC], CP, ROUND).then_inc(S["s_r%d" % t], 1)
+        elif step[0] == "n":
+            waits("S", "s_r%d" % t)
+            C.activation(T.fn[:, TC * t:TC * t + TC], T.r1[:, TC * t:TC * t + TC], CP, -ROUND).then_inc(S["s_n%d" % t], 1)
+        elif step[0] == "g" and step[2] != "e":
+            waits("S", "v_lv", own_v[t])
+            C.activation(m_of(step[2], t, 4), v_at(t, step[2]), CP).then_inc(S["s_v" + step[2]], 1)
+        elif step[0] == "g":
+            waits("S", "v_lv", own_v[t], "s_h%d" % t, *again[:1])
+            C.activation(T.gi[:, t - 2, 1:256:2], v_at(t, "e"), CP).then_inc(S["s_g%d" % t], 1)
+        elif step[0] == "e":
+            waits("S", "v_ld", "v_hz", own_d[t], "v_h%d" % t, *again)
+            C.activation(T.gi[:, t - 2, 0:256:2], d_at(t, "e"), CP).then_inc(S["s_g%d" % t], 1)
+        elif step[0] == "h":
+            waits("S", "t_h%d" % t)
+            C.activation(T.vw[:, t, TC:ring], pv[t][:, 128 - hc:128], CP).then_inc(S["s_h%d" % t], 1)
+        elif step == "ye0":
+            waits("S", "t_oe0")
+            for h in range(2):
+                C.activation(T.ye[:, 0:2, h:32:2], pv[0][:, h:128:4], CP).then_inc(S.s_ye, 1)
+        elif step[0] == "y":
+            r = step[1]
+            c0, c1, j0, j1 = own_y[r]
+            waits("S", "t_o%s%d" % (r, t))
+            for h in range(2):
+                C.activation(T.ys[:, TC * t + j0 + h:TC * t + j1:2], banks[r][t][:, c0 + h:c1:4], CP).then_inc(S["s_" + step], 1)
+        elif step == "se":
+            waits("S", "v_y:2")
+            C.dma_start(T.y[:, 2 * TC - H:2 * TC], T.ye[:, 2, :]).then_inc(S.st2, 16)
+
+    def sync(step):
+        if step == "se0":
+            waits("Y", "s_ye:2")
+            Y.dma_start(T.y[:, 0:H], T.ye[:, 1, :]).then_inc(S.st1, 16)
+        elif step == "se1":
+            waits("Y", "s_ye:2", "v_y:2")
+            Y.dma_start(T.y[:, TC - H:TC + H], T.ye[:, 0:4:3, :]).then_inc(S.st1, 16)
+        else:
+            r, o = step[1], int(step[2])
+            waits("Y", "s_y%s%d:2" % (r, o))
+            a, e = TC * o + own_y[r][2], TC * o + own_y[r][3]
+            Y.dma_start(T.y[:, a:e], T.ys[:, a:e]).then_inc(S.st1, 16)
+
+    C.dma_start(T.xt[:, 4 * EL:512], T.x[:, 0:512 - 4 * EL]).then_inc(S.d_xe, 16)
+    Y.dma_start(T.ub[:], T.u[:, 0:64]).then_inc(S.d_u, 16)
+    Y.dma_start(T.xt[:, 0:4 * EL], T.x[:, 4 * ROT:4 * TC]).then_inc(S.d_xe, 16)
+    Y.dma_start(T.xt[:, 512:1024], T.x[:, 512 - 4 * EL:4 * ROT]).then_inc(S.d_x, 16)
+    for q, run in (("G", gpsimd), ("V", vector), ("T", tensor), ("S", scalar), ("Y", sync)):
+        for step in ORDER[q].split():
+            run(step)
+    waits("G", "loc:%d" % sum(2 * len(q[3]) for q in out))
+    waits("S", "st2:16")
+    waits("Y", "st1:%d" % (16 * len(ORDER["Y"].split())))

@@ -4,16 +4,17 @@ from concourse.mybir import dt, AluOpType, ActivationFunctionType
 H, TC, CL = 32, 256, 31
 ROT = 160
 EL = TC - ROT
+X0, LEAD = 16, 6
 ROUND = 1.5 * 2.0 ** 23
-RUNS = {"a": (16, 32), "b": (0, 8), "e": (8, 16)}
+RUNS = {"a": (0, 12), "b": (12, 24), "e": (24, 32)}
 ORDER = {
-    "G": "part eye cols send w zeros vdup ddup add_a add_b",
-    "V": "fill bits m1 eye2 eye3 qe hs qx qz eye0 eye1 qu d2 d3 dl nl w eq end lv wz d0 ld d1 fr0 fr1 "
-         "p2a p3a p0a p1a p2b p3b p0b p1b qw h2 h3 h0 h1 hx p0e p1e scan2 scan3 qa m0e m1e qb qe2 ye1",
-    "T": "v2 v3 list v0 v1 f0 f1 h2 h3 h0 h1 oa ob oe",
-    "S": "zt u1 u2 m0 u3 tab1 u4 tab2 v2 tab3 v3 pick v0 v1 r0 r1 n0 n1 g2a g3a g0a g1a g2b g3b g0b g1b h2 h3 h0 h1 "
-         "g2e g3e e2 e3 ya0 ya1 yb0 yb1 ye0 se",
-    "Y": "sa0 sa1 sb0 sb1 se0 se1",
+    "G": "eye part cols w1 send ddup add_a vdup add_b",
+    "V": "fill ones bits eye2 eye3 m1 eye0 hs qe qz eye1 u3 qx db2 db3 db0 qu dl db1 nl da2 w eq da3 end da0 lv wz fa0 ld fa1 da1 "
+         "p2a p3a p0a fb0 fb1 p1a p2b p3b p0b p1b qw1 h2 h3 h0 h1 hx qw0 p0e p1e scan2 scan3 qa m0e m1e qe2 qb ye1 yb1",
+    "T": "vb2 vb3 vb0 lb la vb1 va2 va3 va0 fa0 fa1 va1 fb0 fb1 h2 h3 h0 h1 oa oe ob",
+    "S": "zeros nil u1 zt m0 u2 tab vb2 vb3 vb0 u4 lb la vb1 va2 va3 va0 ra0 ra1 na0 va1 na1 g2a g3a rb0 rb1 nb0 nb1 g0a g1a "
+         "g2b g3b g0b g1b h2 h3 h0 h1 g2e g3e e2 e3 ya0 ya1 ye0 se3 yb0 sb0",
+    "Y": "w0 sa0 sa1 se0 se4 sb1",
 }
 SCRATCH = {
     "ub": ("sbuf", [128, 2, 8, 4], "bfloat16"),
@@ -21,25 +22,25 @@ SCRATCH = {
     "zt": ("sbuf", [128, 9, 16, 4], "bfloat16"),
     "vw": ("sbuf", [128, 4, 384], "float32"),
     "dw": ("sbuf", [128, 4, 392], "float32"),
-    "zf": ("sbuf", [128, 1024], "float32"),
-    "gi": ("sbuf", [128, 2, 256], "float32"),
+    "gi": ("sbuf", [128, 4, 512], "float32"),
+    "tm": ("sbuf", [128, 2, 512], "bfloat16"),
     "pr": ("sbuf", [128, 512, 4], "float32"),
-    "mt": ("sbuf", [128, 4 * 514], "bfloat16"),
-    "ye": ("sbuf", [128, 4, 32], "float32"),
+    "ys": ("sbuf", [128, 16, 32], "float32"),
 }
-for names, width, kind in (("rq", H, "q"), ("qx", 320, "q"), ("qu", 256, "q"), ("qz", 144, "q"), ("qi qw", 512, "q"), ("qm", 514, "q"),
-                           ("rs", H, "s"), ("sx", 320, "s"), ("su", 256, "s"), ("sz", 144, "s"), ("si sw", 512, "s"), ("sm", 514, "s"),
-                           ("xt", 1024, "b"), ("eye", 516, "b"), ("wb", 2048, "b"),
-                           ("pi b0 b1", 1, "i"), ("nl", 32, "i"), ("m0 m1 hs", 1, "f"),
-                           ("ic tab pa pb dl dc eq wl wz", 32, "f"), ("lv ld", 32, "u"), ("r1 fn ys", 512, "f"),
+for names, width, kind in (("rq", H, "q"), ("qx", 336, "q"), ("qu", 256, "q"), ("qz", 144, "q"), ("qi qw", 512, "q"), ("qm", 514, "q"),
+                           ("rs", H, "s"), ("sx", 336, "s"), ("su", 256, "s"), ("sz", 144, "s"), ("si sw", 512, "s"), ("sm", 514, "s"),
+                           ("xt", 4 * (TC + LEAD), "b"), ("eye", 516, "b"), ("nil", 192, "b"), ("wb", 2048, "b"), ("mt", 4 * 514, "b"),
+                           ("pi b0 b1", 1, "i"), ("nl", 32, "i"), ("m0 m1 hs", 1, "f"), ("dg", 128, "f"), ("zf", 1024, "f"),
+                           ("ic tab pa pb dl dc eq wl wz", 32, "f"), ("lv ld", 32, "u"), ("r1 fn", 512, "f"),
                            ("pf0 pf1 pl px pv0 pv1 pv2 pv3", 512, "p")):
     for name in names.split():
         SCRATCH[name] = ("psum" if kind == "p" else "sbuf", [128, width],
                          {"q": "float8_e4m3fn_x4", "s": "uint8", "b": "bfloat16", "i": "int32", "u": "uint16"}.get(kind, "float32"))
-SEMAPHORES = ("d_xe d_u d_x d_w d_ma d_mb st1 st2 ra rb arr loc g_p g_c g_e g_z g_vd g_dd v_eye v_zt v_hz v_b v_m1 v_hs v_qe v_qx v_qz v_qu "
-              "v_dl v_nl v_dc v_eq v_wl v_we v_wz v_lv v_ld v_f0 v_f1 v_pa v_pb v_pe v_qw v_qa v_qb v_qe2 v_dx v_se v_me v_y "
-              "s_zt s_u1 s_u2 s_u3 s_u4 s_m0 s_tab s_tb3 s_p s_r0 s_r1 s_n0 s_n1 s_va s_vb s_g2 s_g3 s_ya0 s_ya1 s_yb0 s_yb1 s_ye t_f0 t_f1 t_l "
-              "t_oa0 t_oa1 t_ob0 t_ob1 t_oe0 t_oe1").split() + [p + str(b) for p in ("v_e", "s_v", "s_h", "v_d", "v_h", "t_v", "t_h") for b in range(4)]
+SEMAPHORES = ("d_xe d_u d_x d_w0 d_w1 d_ma d_mb st1 st2 ra rb arr loc g_p g_c g_e g_vd g_dd v_eye v_zt v_one v_b v_m1 v_hs v_qe v_qx v_qz v_qu "
+              "v_dl v_nl v_dc v_eq v_wl v_we v_wz v_lv v_ld v_pa v_pb v_pe0 v_pe1 v_qw v_qa v_qb v_qe2 v_dx v_me "
+              "s_nil s_z s_zt s_u1 s_u2 s_u3 s_u4 s_m0 s_tab s_p s_ga s_gb t_la t_lb").split()
+SEMAPHORES += [p + str(b) for p in "v_e v_s s_g s_va s_vb s_h v_da v_db v_h t_va t_vb t_h".split() for b in range(4)]
+SEMAPHORES += [p + str(b) for p in "v_fa v_fb s_ra s_rb s_na s_nb s_ya s_yb s_ye t_fa t_fb t_oa t_ob t_oe".split() for b in range(2)]
 
 
 def mask_of(engines):
@@ -56,8 +57,8 @@ def routes(T, topo, core):
         cand = [c for c in topo.cores_of(core) if c != core and topo.may_write(c, dst)]
         cand.sort(key=lambda c: (topo.die(c) != topo.die(core), c))
         relay = cand[side]
-        out.append((side, relay, dst, topo.engines(core, relay)[4 * side:4 * side + 4], topo.engines(relay, dst)[::2], EL - H * side,
-                    TC + (H if side == 1 and nb < n - 1 else 0)))
+        out.append((side, relay, dst, topo.engines(core, relay)[4 * side:4 * side + 4], topo.engines(relay, dst)[::2], X0 + EL - H * side,
+                    X0 + TC + (H if side == 1 and nb < n - 1 else 0)))
     return out
 
 
@@ -89,11 +90,14 @@ def rank_program(g, core, T, topo):
     V, C, P, Y = g.vector, g.scalar, g.tensor, g.sync
     pv, pf = [T["pv%d" % b] for b in range(4)], [T.pf0, T.pf1]
     banks = {"a": pf, "b": [T.pl, T.px], "e": [pv[0], pv[2]]}
+    lists = {"a": T.pl, "b": T.px}
     hc = H if end else 2 * H
     ring = TC + hc
-    wide = TC + H - 1 if first else ring + 2 * H - 1
+    wide = {"a": TC - 1, "b": TC - 1, "e": TC + H - 1 if first else ring + 2 * H - 1}
     again = [] if first else ["g_vd", "g_dd", "v_dx"]
-    own_v, own_d = ["s_v%d:2" % t for t in range(4)], ["v_d%d:2" % t for t in range(4)]
+    e0, e1 = RUNS["e"]
+    back = {r: 2 if r != "e" and RUNS[r][1] - RUNS[r][0] == 8 else 0 for r in RUNS}
+    half = {"a": 128, "b": 0}
     out = routes(T, topo, core)
     arrivals = sum(2 * len(q[4]) for nb in (rank - 1, rank + 1) if 0 <= nb < n for q in routes(T, topo, T.cores[nb]) if q[2] == core)
     seen = {}
@@ -109,28 +113,28 @@ def rank_program(g, core, T, topo):
         return slice(16 * RUNS[r][0], 16 * RUNS[r][1])
 
     def m_of(r, t=0, every=1):
-        return T.mt[:, 8 + 64 * RUNS[r][0] + t:8 + 64 * RUNS[r][1]:every]
-
-    def fr_of(r):
-        return T.zf[:, 32 * RUNS[r][0] + 1:32 * RUNS[r][1]:2]
+        return T.mt[:, 64 * RUNS[r][0] + t:64 * RUNS[r][1]:every]
 
     def v_at(t, r):
-        return T.vw[:, t, 0:wide if r == "e" else TC - 1].indirect(T.lv[:, RUNS[r][0]:RUNS[r][1]])
+        return T.vw[:, t, 0:wide[r]].indirect(T.lv[:, RUNS[r][0]:RUNS[r][1]])
 
     def d_at(t, r):
-        return T.dw[:, t, 0:1 + (wide if r == "e" else TC - 1)].indirect(T.ld[:, RUNS[r][0]:RUNS[r][1]])
+        return T.dw[:, t, 0:1 + wide[r]].indirect(T.ld[:, RUNS[r][0]:RUNS[r][1]])
 
-    def zeros(ap, count):
-        return g.iota(ap, [[0, count]], 0, 0, allow_small_or_imprecise_dtypes=True)
+    def y_out(q, call, r, o):
+        waits(q, "t_o%s%d" % (r, o))
+        a, e = RUNS[r]
+        for h in range(2):
+            call(T.ys[:, 8 * o + a // 4:8 * o + e // 4, h:32:2], banks[r][o][:, back[r] + h:16 * (e - a) + back[r] - 2:4]).then_inc(S["s_y%s%d" % (r, o)], 1)
 
     def gpsimd(step):
         if step == "part":
             g.iota(T.pi[:], [[0, 1]], 0, 1).then_inc(S.g_p, 1)
         elif step == "eye":
-            waits("G", "v_eye")
-            g.affine_select(T.eye[:, 0:516:4], T.eye[:, 0:516:4], [[-1, 129]], A.not_equal, 1.0, 1, 1).then_inc(S.g_e, 1)
+            g.iota(T.dg[:], [[1, 128]], 0, -1, allow_small_or_imprecise_dtypes=True).then_inc(S.g_e, 1)
         elif step == "cols":
-            g.iota(T.ic[:], [[8, 32]], 1, 0, allow_small_or_imprecise_dtypes=True).then_inc(S.g_c, 1)
+            g.iota(T.ic[:, 0:28], [[8, 28]], 1 + H, 0, allow_small_or_imprecise_dtypes=True).then_inc(S.g_c, 1)
+            g.iota(T.ic[:, 28:32], [[8, 4]], 1 + (0 if first else ring), 0, allow_small_or_imprecise_dtypes=True).then_inc(S.g_c, 1)
         elif step == "send":
             waits("G", "v_qe")
             codes, planes = [], []
@@ -143,29 +147,38 @@ def rank_program(g, core, T, topo):
                                                 src=T.sx[:, col:col + H], dst=T.rs[:, 0:H]))
             g.remote_dma_fused(codes, local_sem=S.loc)
             g.remote_dma_fused(planes, local_sem=S.loc)
-        elif step == "w":
-            waits("G", "d_x:16")
-            g.dma_start(T.wb[:], T.w[:]).then_inc(S.d_w, 16)
-        elif step == "zeros":
-            zeros(T.mt[:, 0:8], 8).then_inc(S.g_z, 1)
-            zeros(T.zf[:, 32 * RUNS["e"][0]:32 * RUNS["e"][1]:2], 128).then_inc(S.g_z, 1)
-        elif step == "vdup" and not first:
-            waits("G", *own_v)
-            g.affine_select(T.vw[:, :, ring:ring + 2 * H], T.vw[:, :, 0:2 * H], [[0, 8 * H]], A.is_equal, 0.0, 0, 0).then_inc(S.g_vd, 1)
-        elif step == "ddup" and not first:
-            waits("G", *own_d)
-            g.affine_select(T.dw[:, :, 1 + ring:1 + ring + 2 * H], T.dw[:, :, 1:1 + 2 * H], [[0, 8 * H]], A.is_equal, 0.0, 0, 0).then_inc(S.g_dd, 1)
+        elif step[0] == "w":
+            k = int(step[1])
+            g.dma_start(T.wb[:, 4 * TC * k:4 * TC * (k + 1)], T.w[:, 4 * TC * k:4 * TC * (k + 1)]).then_inc(S["d_w%d" % k], 16)
+        elif step == "vdup":
+            if not first:
+                waits("G", "s_va0", "s_va1", "s_va2", "s_va3")
+                g.affine_select(T.vw[:, :, ring:ring + 2 * H], T.vw[:, :, 0:2 * H], [[0, 8 * H]], A.is_equal, 0.0, 0, 0).then_inc(S.g_vd, 1)
+        elif step == "ddup":
+            if not first:
+                waits("G", "v_da0", "v_da1", "v_da2", "v_da3")
+                g.affine_select(T.dw[:, :, 1 + ring:1 + ring + 2 * H], T.dw[:, :, 1:1 + 2 * H], [[0, 8 * H]], A.is_equal, 0.0, 0, 0).then_inc(S.g_dd, 1)
         elif step[:3] == "add":
             r = step[4]
-            waits("G", "v_p%s:4" % r, "s_v%s:4" % r)
+            waits("G", "v_p%s:4" % r, "s_g%s:4" % r)
             g.dma_start(m_of(r), T.pr[:, words(r), :], accum_op=A.add).then_inc(S["d_m" + r], 16)
 
     def vector(step):
         t = int(step[-1]) if step[-1].isdigit() else int(step[1]) if step[1:2].isdigit() else None
         if step == "fill":
+            V.memset(T.nil[:], 0.0).then_inc(S.v_zt, 1)
             V.memset(T.eye[:], 0.0).then_inc(S.v_eye, 1)
-            V.memset(T.zt[:], 0.0).then_inc(S.v_zt, 1)
-            V.memset(T.dw[:, :, 0:TC + 1:TC] if last else T.dw[:, :, 0], 0.0).then_inc(S.v_hz, 1)
+        elif step == "ones":
+            waits("V", "v_eye", "g_e")
+            V.tensor_scalar(T.eye[:, 4:516:4], T.dg[:], 0.0, None, A.is_equal).then_inc(S.v_one, 1)
+        elif step[0] == "u":
+            waits("V", "s_u1:2", "s_u%d" % (t - 1))
+            c = 2 ** (t - 1)
+            V.tensor_copy(T.us[:, :, :, c:2 * c, :], T.us[:, :, :, 0:c, :]).then_inc(S["s_u%d" % t], 1)
+        elif step[0] == "r":
+            a = half[step[1]]
+            waits("V", "t_f" + step[1:])
+            V.tensor_scalar(T.fn[:, TC * t + a:TC * t + a + 128], pf[t][:, 0:128], ROUND, -ROUND, A.add, A.add).then_inc(S["s_n" + step[1:]], 1)
         elif step == "bits":
             waits("V", "g_p")
             V.tensor_scalar(T.b0[:], T.pi[:], 1, None, A.bitwise_and).then_inc(S.v_b, 1)
@@ -177,32 +190,32 @@ def rank_program(g, core, T, topo):
             waits("V", "v_m1")
             V.tensor_scalar(T.hs[:], T.b1[:], T.m1[:], None, A.add).then_inc(S.v_hs, 1)
         elif step[:3] == "eye":
-            waits("V", "g_e")
+            waits("V", "v_one")
             V.quantize_mx(T.qi[:, 128 * t:128 * t + 128], T.si[:, 128 * t:128 * t + 128], T.eye[:, 4 - t:516 - t]).then_inc(S["v_e%d" % t], 1)
         elif step == "qe":
             waits("V", "d_xe:32")
-            V.quantize_mx(T.qx[:, 0:128], T.sx[:, 0:128], T.xt[:, 0:512]).then_inc(S.v_qe, 1)
+            V.quantize_mx(T.qx[:, X0 - LEAD:X0 + 128], T.sx[:, X0 - LEAD:X0 + 128], T.xt[:, 0:4 * (LEAD + 128)]).then_inc(S.v_qe, 1)
         elif step == "qx":
             waits("V", "d_x:16")
-            V.quantize_mx(T.qx[:, 128:256], T.sx[:, 128:256], T.xt[:, 512:1024]).then_inc(S.v_qx, 1)
+            V.quantize_mx(T.qx[:, X0 + 128:X0 + TC], T.sx[:, X0 + 128:X0 + TC], T.xt[:, 4 * (LEAD + 128):4 * (LEAD + TC)]).then_inc(S.v_qx, 1)
         elif step == "qz":
             waits("V", "s_zt:4")
             V.quantize_mx(T.qz[:], T.sz[:], T.zt[:]).then_inc(S.v_qz, 1)
         elif step == "qu":
             waits("V", "s_u4")
             V.quantize_mx(T.qu[:], T.su[:], T.us[:]).then_inc(S.v_qu, 1)
-        elif step == "qw":
-            waits("V", "d_w:16")
-            V.quantize_mx(T.qw[:], T.sw[:], T.wb[:]).then_inc(S.v_qw, 1)
+        elif step[:2] == "qw":
+            waits("V", "d_w%d:16" % t)
+            V.quantize_mx(T.qw[:, TC * t:TC * t + TC], T.sw[:, TC * t:TC * t + TC], T.wb[:, 4 * TC * t:4 * TC * (t + 1)]).then_inc(S.v_qw, 1)
         elif step == "dl":
-            waits("V", "s_p:2")
+            waits("V", "s_p:4")
             V.tensor_tensor(T.dl[:], T.pa[:], T.pb[:], A.add).then_inc(S.v_dl, 1)
         elif step == "nl":
             waits("V", "v_dl")
             V.tensor_scalar(T.nl[:], T.dl[:], -float(CL), float(CL), A.max, A.min).then_inc(S.v_nl, 1)
             V.tensor_scalar(T.dc[:], T.dl[:], -float(CL), float(CL), A.max, A.min).then_inc(S.v_dc, 1)
         elif step == "w":
-            waits("V", "v_nl", "s_tb3")
+            waits("V", "v_nl", "s_tab")
             V.tensor_tensor(T.wl[:], T.nl[:], T.tab[:], A.add).then_inc(S.v_wl, 1)
         elif step == "eq":
             waits("V", "v_dc")
@@ -210,7 +223,7 @@ def rank_program(g, core, T, topo):
         elif step == "end":
             if end:
                 waits("V", "v_wl")
-                wl = T.wl[:, 8:12] if last else T.wl[:]
+                wl = T.wl[:, 24:28] if last else T.wl[:, 28:32]
                 V.tensor_scalar(wl, wl, float(TC) if last else 1.0, None, A.min if last else A.max).then_inc(S.v_we, 1)
         elif step == "lv":
             waits("V", "v_we" if end else "v_wl")
@@ -221,19 +234,26 @@ def rank_program(g, core, T, topo):
         elif step == "ld":
             waits("V", "v_wz")
             V.tensor_copy(T.ld[:], T.wz[:]).then_inc(S.v_ld, 1)
-        elif step[0] == "d":
-            waits("V", own_v[t])
-            V.tensor_tensor(T.dw[:, t, 1:ROT], pv[t][:, EL + 1:TC], T.vw[:, t, 0:ROT - 1], A.subtract).then_inc(S["v_d%d" % t], 1)
-            V.tensor_tensor(T.dw[:, t, ROT:TC], pv[t][:, 0:EL], T.vw[:, t, ROT - 1:TC - 1], A.subtract).then_inc(S["v_d%d" % t], 1)
-        elif step[:2] == "fr":
-            waits("V", "s_n%d" % t)
+        elif step[:2] == "da":
+            waits("V", "s_va%d" % t)
+            V.tensor_tensor(T.dw[:, t, 1:1 + ROT], T.vw[:, t, 1:1 + ROT], pv[t][:, 0:ROT], A.subtract).then_inc(S["v_da%d" % t], 1)
+        elif step[:2] == "db":
+            waits("V", "s_vb%d" % t)
+            V.tensor_tensor(T.dw[:, t, 1 + ROT:TC], T.vw[:, t, 1 + ROT:TC], pv[t][:, 0:EL - 1], A.subtract).then_inc(S["v_db%d" % t], 1)
+        elif step == "fill":
+            pass
+        elif step[0] == "f":
+            a = half[step[1]]
+            z = 4 * (128 - a)
+            waits("V", "s_n" + step[1:])
             for h in range(2):
-                V.tensor_tensor(T.zf[:, 4 * t + 2 * h + 1:1024:8], pf[t][:, h:TC:2], T.fn[:, TC * t + h:TC * t + TC:2],
-                                A.subtract).then_inc(S["v_f%d" % t], 1)
+                V.tensor_tensor(T.zf[:, z + 4 * t + 2 * h + 1:z + 512:8], pf[t][:, h:128:2], T.fn[:, TC * t + a + h:TC * t + a + 128:2],
+                                A.subtract).then_inc(S["v_" + step], 1)
         elif step[0] == "p":
             r = step[2]
-            waits("V", "v_ld", "v_hz", "v_f0:2", "v_f1:2", own_d[t], *(["v_h%d" % t] + again if r == "e" else []))
-            V.tensor_tensor(T.pr[:, words(r), t], d_at(t, r), fr_of(r), A.mult).then_inc(S["v_p" + r], 1)
+            waits("V", "v_ld", "s_z:3", "v_fa0:2", "v_fa1:2", "v_da%d" % t, "v_db%d" % t, *([] if r == "a" else ["v_fb0:2", "v_fb1:2"]))
+            waits("V", *(["v_h%d" % t] + again if r == "e" else []))
+            V.tensor_tensor(T.pr[:, words(r), t], d_at(t, r), T.zf[:, 32 * RUNS[r][0] + 1:32 * RUNS[r][1]:2], A.mult).then_inc(S["v_pe%d" % t if r == "e" else "v_p" + r], 1)
         elif step == "hx":
             if not first:
                 waits("V", "s_h0", "s_h1", "s_h2", "s_h3")
@@ -243,55 +263,87 @@ def rank_program(g, core, T, topo):
             waits("V", "s_h%d" % t)
             V.tensor_tensor(T.dw[:, t, 1 + a:ring], pv[t][:, 128 - (ring - 1 - a):128], T.vw[:, t, a:ring - 1], A.subtract).then_inc(S["v_h%d" % t], 1)
         elif step[:4] == "scan":
-            waits("V", "g_z:2", "s_g%d:2" % t)
-            V.tensor_tensor_scan(m_of("e", t - 2, 2), T.zf[:, 32 * RUNS["e"][0]:32 * RUNS["e"][1]], T.gi[:, t - 2], 0.0,
-                                 A.mult, A.add).then_inc(S.v_se, 1)
+            waits("V", "s_z:3", "s_g%d:2" % t, "v_fb0:2", "v_fb1:2")
+            V.tensor_tensor_scan(m_of("e", t - 2, 2) if t > 1 else T.tm[:, t, 0:32 * (e1 - e0)], T.zf[:, 32 * e0:32 * e1],
+                                 T.gi[:, t, 0:32 * (e1 - e0)], 0.0, A.mult, A.add).then_inc(S["v_s%d" % t], 1)
         elif step[0] == "m":
-            waits("V", "v_pe:2", "v_se:2")
+            waits("V", "v_pe%d" % t, "v_s%d" % (t + 2))
             V.tensor_tensor(m_of("e", t, 4), v_at(t, "e"), T.pr[:, words("e"), t], A.add).then_inc(S.v_me, 1)
+        elif step[0] == "c":
+            waits("V", "v_s%d" % t, "v_s%d" % (t + 2))
+            V.tensor_copy(m_of("e", t, 4), T.tm[:, t, 1:32 * (e1 - e0):2]).then_inc(S.v_me, 1)
         elif step[0] == "q":
             r = step[1]
-            waits("V", *{"a": ["d_ma:16"], "b": ["d_mb:16", "g_z:2"], "e": ["v_me:2"]}[r])
-            a, e = (0 if r == "b" else 2 + 16 * RUNS[r][0]), 2 + 16 * RUNS[r][1]
+            waits("V", "v_me:2" if r == "e" else "d_m%s:16" % r)
+            a, e = 16 * RUNS[r][0], 16 * RUNS[r][1] + (2 if r == "e" else 0)
             V.quantize_mx(T.qm[:, a:e], T.sm[:, a:e], T.mt[:, 4 * a:4 * e]).then_inc(S["v_" + step], 1)
-        elif step == "ye1":
-            waits("V", "t_oe1")
-            for h in range(2):
-                V.tensor_copy(T.ye[:, 2:4, h:32:2], pv[2][:, h:128:4]).then_inc(S.v_y, 1)
+        elif step[0] == "y":
+            y_out("V", V.tensor_copy, step[1], t)
 
     def mm(o, cols, lq, ls, a, rq, rs, c, start, stop):
         return P.matmul_mx(o[:, 0:cols], lq[:, a:a + 128], ls[:, a:a + 128], rq[:, c:c + cols], rs[:, c:c + cols], start, stop)
 
     def tensor(step):
-        t = int(step[1]) if step[1].isdigit() else None
-        if step[0] == "v":
-            waits("T", "v_qe", "v_qx", "v_e%d" % t)
-            mm(pv[t], TC, T.qi, T.si, 128 * t, T.qx, T.sx, 0, True, True).then_inc(S["t_v%d" % t], 1)
-        elif step == "list":
-            waits("T", "v_qz")
+        t = int(step[-1]) if step[-1].isdigit() else None
+        if step[:2] == "va":
+            waits("T", "v_qx", "v_db%d" % t)
+            mm(pv[t], ROT, T.qi, T.si, 128 * t, T.qx, T.sx, X0 + EL, True, True).then_inc(S["t_va%d" % t], 1)
+        elif step[:2] == "vb":
+            waits("T", "v_qe", "v_e%d" % t)
+            mm(pv[t], 128, T.qi, T.si, 128 * t, T.qx, T.sx, X0, True, True).then_inc(S["t_vb%d" % t], 1)
+        elif step[0] == "l":
+            waits("T", "v_qz", "v_qe", *(["v_qx"] if step == "la" else []))
             for h in range(4):
-                r = mm(T.pl, TC - 6, T.qz, T.sz, 12 - 4 * h, T.qx, T.sx, 2 * h, h == 0, h == 3)
-            r.then_inc(S.t_l, 1)
+                r = mm(lists[step[1]], 128, T.qz, T.sz, 12 - 4 * h, T.qx, T.sx, X0 - LEAD + half[step[1]] + 2 * h, h == 0, h == 3)
+            r.then_inc(S["t_" + step], 1)
         elif step[0] == "f":
-            waits("T", "v_qu")
-            mm(pf[t], TC, T.qu, T.su, 128 * t, T.qx, T.sx, 0, True, True).then_inc(S["t_f%d" % t], 1)
+            waits("T", "v_qu", "v_qe", "v_qx", *(["v_fa%d:2" % t] if step[1] == "b" else []))
+            mm(pf[t], 128, T.qu, T.su, 128 * t, T.qx, T.sx, X0 + half[step[1]], True, True).then_inc(S["t_" + step], 1)
         elif step[0] == "h":
-            waits("T", "arr:%d" % arrivals, own_d[t])
-            mm(pv[t], 128, T.qi, T.si, 128 * t, T.qx, T.sx, ring - 128, True, True).then_inc(S["t_h%d" % t], 1)
+            waits("T", "arr:%d" % arrivals, "v_da%d" % t)
+            mm(pv[t], 128, T.qi, T.si, 128 * t, T.qx, T.sx, X0 + ring - 128, True, True).then_inc(S["t_h%d" % t], 1)
         else:
             r = step[1]
-            waits("T", "v_qw", "v_f0:2", "v_f1:2", "s_p:2", *{"a": ["v_qa"], "b": ["v_qb"], "e": ["v_qa", "v_qe2"]}[r])
-            a, cols = {"a": (2 + 16 * RUNS[r][0], 254), "b": (0, 128), "e": (2 + 16 * RUNS[r][0], 128)}[r]
+            waits("T", "v_qw:2", "v_fb0:2", "v_fb1:2", "s_p:4", "v_qe2" if r == "e" else "v_q" + r, *(["v_qa"] if back[r] else []))
+            a = 16 * RUNS[r][0] - back[r]
+            cols = max(128, 16 * (RUNS[r][1] - RUNS[r][0]) - 2)
             for o in range(2):
                 mm(banks[r][o], cols, T.qw, T.sw, 128 * o, T.qm, T.sm, a, True, False)
                 mm(banks[r][o], cols, T.qw, T.sw, 256 + 128 * o, T.qm, T.sm, a + 2, False, True).then_inc(S["t_o%s%d" % (r, o)], 1)
 
-    own_y = {"a": (0, 254, H, ROT), "b": (2, 128, ROT, TC - H)}
+    def store(q, call, step, sem):
+        if step[0] == "w":
+            k = int(step[1])
+            call(T.wb[:, 4 * TC * k:4 * TC * (k + 1)], T.w[:, 4 * TC * k:4 * TC * (k + 1)]).then_inc(S["d_w%d" % k], 16)
+            return
+        r, o = step[1], int(step[2])
+        a, e = RUNS[r]
+        if r != "e":
+            waits(q, "s_y%s%d:2" % (r, o))
+            call(T.y[:, TC * o + H + 8 * a:TC * o + H + 8 * e], T.ys[:, 8 * o + a // 4:8 * o + e // 4, :]).then_inc(sem, 16)
+        elif o < 2:
+            waits(q, "s_ye%d:2" % o)
+            call(T.y[:, TC * o:TC * o + H], T.ys[:, 8 * o + 7, :]).then_inc(sem, 16)
+        elif o < 4:
+            waits(q, "s_ye%d:2" % (o - 2))
+            call(T.y[:, TC * (o - 2) + H + 8 * a:TC * (o - 1)], T.ys[:, 8 * (o - 2) + a // 4:8 * (o - 2) + 7, :]).then_inc(sem, 16)
+        else:
+            waits(q, "s_ye0:2", "s_ye1:2")
+            call(T.y[:, TC - H:TC + H], T.ys[:, 6:16:9, :]).then_inc(sem, 16)
 
     def scalar(step):
         t = int(step[-1]) if step[-1].isdigit() else int(step[1]) if step[1:2].isdigit() else None
-        if step == "zt":
-            waits("S", "v_zt", "d_u:16")
+        if step == "nil":
+            waits("S", "v_zt")
+            for i in range(4):
+                C.activation(T.zt[:, :, 4 * i:4 * i + 4, :], T.nil[:, 0:144], CP).then_inc(S.s_nil, 1)
+        elif step == "zeros":
+            waits("S", "v_zt")
+            C.activation(T.dw[:, :, 0:TC + 1:TC] if last else T.dw[:, :, 0], T.nil[:, 0:8 if last else 4], CP).then_inc(S.s_z, 1)
+            C.activation(T.mt[:, 2048:2056], T.nil[:, 0:8], CP).then_inc(S.s_z, 1)
+            C.activation(T.zf[:, 32 * e0:32 * e1:2], T.nil[:, 0:16 * (e1 - e0)], CP).then_inc(S.s_z, 1)
+        elif step == "zt":
+            waits("S", "s_nil:4", "d_u:16")
             for k in range(2):
                 for e in range(2):
                     C.activation(T.zt[:, 0:8, 12 + 2 * k + e, :], T.ub[:, k, :, :], CP).then_inc(S.s_zt, 1)
@@ -306,75 +358,52 @@ def rank_program(g, core, T, topo):
         elif step == "m0":
             waits("S", "v_m1")
             C.activation(T.m0[:], T.m1[:], CP, 1.0, -1.0).then_inc(S.s_m0, 1)
-        elif step == "tab1":
-            waits("S", "v_hs", "g_c")
-            C.activation(T.tab[:, 0:12], T.ic[:, 20:32], ID, T.hs[:]).then_inc(S.s_tab, 1)
-        elif step == "tab2":
-            waits("S", "v_hs", "g_c")
-            C.activation(T.tab[:, 12:32], T.ic[:, 0:20], ID, T.hs[:]).then_inc(S.s_tab, 1)
-        elif step == "tab3":
-            waits("S", "s_tab:2")
-            C.activation(T.tab[:, 12:16], T.tab[:, 12:16], CP, 0.0 if first else float(ring)).then_inc(S.s_tb3, 1)
-        elif step[0] == "v":
-            waits("S", "t_v%d" % t)
-            C.activation(T.vw[:, t, 0:ROT], pv[t][:, EL:TC], CP).then_inc(S["s_v%d" % t], 1)
-            C.activation(T.vw[:, t, ROT:TC], pv[t][:, 0:EL], CP).then_inc(S["s_v%d" % t], 1)
-        elif step == "pick":
-            waits("S", "t_l", "s_m0")
-            C.activation(T.pa[:], T.pl[:, 0:TC - 6:8], CP, 0.0, T.m0[:]).then_inc(S.s_p, 1)
-            C.activation(T.pb[:], T.pl[:, 1:TC - 6:8], CP, 0.0, T.m1[:]).then_inc(S.s_p, 1)
+        elif step == "tab":
+            waits("S", "v_hs", "g_c:2")
+            C.activation(T.tab[:], T.ic[:], ID, T.hs[:]).then_inc(S.s_tab, 1)
+        elif step[:2] == "va":
+            waits("S", "t_va%d" % t)
+            C.activation(T.vw[:, t, 0:ROT], pv[t][:, 0:ROT], CP).then_inc(S["s_va%d" % t], 1)
+        elif step[:2] == "vb":
+            waits("S", "t_vb%d" % t)
+            C.activation(T.vw[:, t, ROT:TC], pv[t][:, 0:EL], CP).then_inc(S["s_vb%d" % t], 1)
+        elif step[0] == "l":
+            waits("S", "t_" + step, "s_m0")
+            z = (128 - half[step[1]]) // 8
+            C.activation(T.pa[:, z:z + 16], lists[step[1]][:, LEAD:128:8], CP, 0.0, T.m0[:]).then_inc(S.s_p, 1)
+            C.activation(T.pb[:, z:z + 16], lists[step[1]][:, LEAD + 1:128:8], CP, 0.0, T.m1[:]).then_inc(S.s_p, 1)
         elif step[0] == "r":
-            waits("S", "t_f%d" % t)
-            C.activation(T.r1[:, TC * t:TC * t + TC], pf[t][:, 0:TC], CP, ROUND).then_inc(S["s_r%d" % t], 1)
+            a = half[step[1]]
+            waits("S", "t_f" + step[1:])
+            C.activation(T.r1[:, TC * t + a:TC * t + a + 128], pf[t][:, 0:128], CP, ROUND).then_inc(S["s_" + step], 1)
         elif step[0] == "n":
-            waits("S", "s_r%d" % t)
-            C.activation(T.fn[:, TC * t:TC * t + TC], T.r1[:, TC * t:TC * t + TC], CP, -ROUND).then_inc(S["s_n%d" % t], 1)
+            a = TC * t + half[step[1]]
+            waits("S", "s_r" + step[1:])
+            C.activation(T.fn[:, a:a + 128], T.r1[:, a:a + 128], CP, -ROUND).then_inc(S["s_" + step], 1)
         elif step[0] == "g" and step[2] != "e":
-            waits("S", "v_lv", own_v[t])
-            C.activation(m_of(step[2], t, 4), v_at(t, step[2]), CP).then_inc(S["s_v" + step[2]], 1)
+            waits("S", "v_lv", "s_va%d" % t, "s_vb%d" % t)
+            C.activation(m_of(step[2], t, 4), v_at(t, step[2]), CP).then_inc(S["s_g" + step[2]], 1)
         elif step[0] == "g":
-            waits("S", "v_lv", own_v[t], "s_h%d" % t, *again[:1])
-            C.activation(T.gi[:, t - 2, 1:256:2], v_at(t, "e"), CP).then_inc(S["s_g%d" % t], 1)
+            waits("S", "v_lv", "s_va%d" % t, "s_vb%d" % t, "s_h%d" % t, *again[:1])
+            C.activation(T.gi[:, t, 1:32 * (e1 - e0):2], v_at(t, "e"), CP).then_inc(S["s_g%d" % t], 1)
         elif step[0] == "e":
-            waits("S", "v_ld", "v_hz", own_d[t], "v_h%d" % t, *again)
-            C.activation(T.gi[:, t - 2, 0:256:2], d_at(t, "e"), CP).then_inc(S["s_g%d" % t], 1)
+            waits("S", "v_ld", "s_z:3", "v_da%d" % t, "v_db%d" % t, "v_h%d" % t, *again)
+            C.activation(T.gi[:, t, 0:32 * (e1 - e0):2], d_at(t, "e"), CP).then_inc(S["s_g%d" % t], 1)
         elif step[0] == "h":
             waits("S", "t_h%d" % t)
             C.activation(T.vw[:, t, TC:ring], pv[t][:, 128 - hc:128], CP).then_inc(S["s_h%d" % t], 1)
-        elif step == "ye0":
-            waits("S", "t_oe0")
-            for h in range(2):
-                C.activation(T.ye[:, 0:2, h:32:2], pv[0][:, h:128:4], CP).then_inc(S.s_ye, 1)
         elif step[0] == "y":
-            r = step[1]
-            c0, c1, j0, j1 = own_y[r]
-            waits("S", "t_o%s%d" % (r, t))
-            for h in range(2):
-                C.activation(T.ys[:, TC * t + j0 + h:TC * t + j1:2], banks[r][t][:, c0 + h:c1:4], CP).then_inc(S["s_" + step], 1)
-        elif step == "se":
-            waits("S", "v_y:2")
-            C.dma_start(T.y[:, 2 * TC - H:2 * TC], T.ye[:, 2, :]).then_inc(S.st2, 16)
+            y_out("S", lambda a, b: C.activation(a, b, CP), step[1], t)
+        elif step[0] == "s":
+            store("S", C.dma_start, step, S.st2)
 
-    def sync(step):
-        if step == "se0":
-            waits("Y", "s_ye:2")
-            Y.dma_start(T.y[:, 0:H], T.ye[:, 1, :]).then_inc(S.st1, 16)
-        elif step == "se1":
-            waits("Y", "s_ye:2", "v_y:2")
-            Y.dma_start(T.y[:, TC - H:TC + H], T.ye[:, 0:4:3, :]).then_inc(S.st1, 16)
-        else:
-            r, o = step[1], int(step[2])
-            waits("Y", "s_y%s%d:2" % (r, o))
-            a, e = TC * o + own_y[r][2], TC * o + own_y[r][3]
-            Y.dma_start(T.y[:, a:e], T.ys[:, a:e]).then_inc(S.st1, 16)
-
-    C.dma_start(T.xt[:, 4 * EL:512], T.x[:, 0:512 - 4 * EL]).then_inc(S.d_xe, 16)
+    C.dma_start(T.xt[:, 4 * (LEAD + EL):4 * (LEAD + 128)], T.x[:, 0:512 - 4 * EL]).then_inc(S.d_xe, 16)
     Y.dma_start(T.ub[:], T.u[:, 0:64]).then_inc(S.d_u, 16)
-    Y.dma_start(T.xt[:, 0:4 * EL], T.x[:, 4 * ROT:4 * TC]).then_inc(S.d_xe, 16)
-    Y.dma_start(T.xt[:, 512:1024], T.x[:, 512 - 4 * EL:4 * ROT]).then_inc(S.d_x, 16)
-    for q, run in (("G", gpsimd), ("V", vector), ("T", tensor), ("S", scalar), ("Y", sync)):
+    Y.dma_start(T.xt[:, 0:4 * (LEAD + EL)], T.x[:, 4 * (ROT - LEAD):4 * TC]).then_inc(S.d_xe, 16)
+    Y.dma_start(T.xt[:, 4 * (LEAD + 128):4 * (LEAD + TC)], T.x[:, 512 - 4 * EL:4 * ROT]).then_inc(S.d_x, 16)
+    for q, run in (("G", gpsimd), ("V", vector), ("T", tensor), ("S", scalar), ("Y", lambda step: store("Y", Y.dma_start, step, S.st1))):
         for step in ORDER[q].split():
             run(step)
     waits("G", "loc:%d" % sum(2 * len(q[3]) for q in out))
-    waits("S", "st2:16")
-    waits("Y", "st1:%d" % (16 * len(ORDER["Y"].split())))
+    waits("S", "st2:%d" % (16 * sum(step[0] == "s" for step in ORDER["S"].split())))
+    waits("Y", "st1:%d" % (16 * sum(step[0] == "s" for step in ORDER["Y"].split())))

from concourse.bass import DstId, RemoteDMATransfer
from concourse.mybir import dt, AluOpType, ActivationFunctionType

H, TC, CL = 32, 256, 31
ROT = 160
EL = TC - ROT
X0, LEAD = 16, 6
ROUND = 1.5 * 2.0 ** 23
RUNS = {"a": (0, 12), "b": (12, 24), "e": (24, 32)}
ORDER = {
    "G": "eye part cols w1 send ddup add_a vdup add_b",
    "V": "fill ones bits eye2 eye3 m1 eye0 hs qe qz eye1 u3 qx db2 db3 db0 qu dl db1 nl da2 w eq da3 end da0 lv wz fa0 ld fa1 da1 "
         "p2a p3a p0a fb0 fb1 p1a p2b p3b p0b p1b qw1 h2 h3 h0 h1 hx qw0 p0e p1e scan2 scan3 qa m0e m1e qe2 qb ye1 yb1",
    "T": "vb2 vb3 vb0 lb la vb1 va2 va3 va0 fa0 fa1 va1 fb0 fb1 h2 h3 h0 h1 oa oe ob",
    "S": "zeros nil u1 zt m0 u2 tab vb2 vb3 vb0 u4 lb la vb1 va2 va3 va0 ra0 ra1 na0 va1 na1 g2a g3a rb0 rb1 nb0 nb1 g0a g1a "
         "g2b g3b g0b g1b h2 h3 h0 h1 g2e g3e e2 e3 ya0 ya1 ye0 se3 yb0 sb0",
    "Y": "w0 sa0 sa1 se0 se4 sb1",
}
SCRATCH = {
    "ub": ("sbuf", [128, 2, 8, 4], "bfloat16"),
    "us": ("sbuf", [128, 2, 8, 16, 4], "bfloat16"),
    "zt": ("sbuf", [128, 9, 16, 4], "bfloat16"),
    "vw": ("sbuf", [128, 4, 384], "float32"),
    "dw": ("sbuf", [128, 4, 392], "float32"),
    "gi": ("sbuf", [128, 4, 512], "float32"),
    "tm": ("sbuf", [128, 2, 512], "bfloat16"),
    "pr": ("sbuf", [128, 512, 4], "float32"),
    "ys": ("sbuf", [128, 16, 32], "float32"),
}
for names, width, kind in (("rq", H, "q"), ("qx", 336, "q"), ("qu", 256, "q"), ("qz", 144, "q"), ("qi qw", 512, "q"), ("qm", 514, "q"),
                           ("rs", H, "s"), ("sx", 336, "s"), ("su", 256, "s"), ("sz", 144, "s"), ("si sw", 512, "s"), ("sm", 514, "s"),
                           ("xt", 4 * (TC + LEAD), "b"), ("eye", 516, "b"), ("nil", 192, "b"), ("wb", 2048, "b"), ("mt", 4 * 514, "b"),
                           ("pi b0 b1", 1, "i"), ("nl", 32, "i"), ("m0 m1 hs", 1, "f"), ("dg", 128, "f"), ("zf", 1024, "f"),
                           ("ic tab pa pb dl dc eq wl wz", 32, "f"), ("lv ld", 32, "u"), ("r1 fn", 512, "f"),
                           ("pf0 pf1 pl px pv0 pv1 pv2 pv3", 512, "p")):
    for name in names.split():
        SCRATCH[name] = ("psum" if kind == "p" else "sbuf", [128, width],
                         {"q": "float8_e4m3fn_x4", "s": "uint8", "b": "bfloat16", "i": "int32", "u": "uint16"}.get(kind, "float32"))
SEMAPHORES = ("d_xe d_u d_x d_w0 d_w1 d_ma d_mb st1 st2 ra rb arr loc g_p g_c g_e g_vd g_dd v_eye v_zt v_one v_b v_m1 v_hs v_qe v_qx v_qz v_qu "
              "v_dl v_nl v_dc v_eq v_wl v_we v_wz v_lv v_ld v_pa v_pb v_pe0 v_pe1 v_qw v_qa v_qb v_qe2 v_dx v_me "
              "s_nil s_z s_zt s_u1 s_u2 s_u3 s_u4 s_m0 s_tab s_p s_ga s_gb t_la t_lb").split()
SEMAPHORES += [p + str(b) for p in "v_e v_s s_g s_va s_vb s_h v_da v_db v_h t_va t_vb t_h".split() for b in range(4)]
SEMAPHORES += [p + str(b) for p in "v_fa v_fb s_ra s_rb s_na s_nb s_ya s_yb s_ye t_fa t_fb t_oa t_ob t_oe".split() for b in range(2)]


def mask_of(engines):
    return sum(1 << e for e in engines)


def routes(T, topo, core):
    r, n = T.rank_of(core), len(T.cores)
    out = []
    for side, nb in ((0, r - 1), (1, r + 1)):
        if not 0 <= nb < n:
            continue
        dst = T.cores[nb]
        cand = [c for c in topo.cores_of(core) if c != core and topo.may_write(c, dst)]
        cand.sort(key=lambda c: (topo.die(c) != topo.die(core), c))
        relay = cand[side]
        out.append((side, relay, dst, topo.engines(core, relay)[4 * side:4 * side + 4], topo.engines(relay, dst)[::2], X0 + EL - H * side,
                    X0 + TC + (H if side == 1 and nb < n - 1 else 0)))
    return out


def relay_program(g, core, T, topo):
    for rc in topo.cores_of(core):
        if T.rank_of(rc) is None:
            continue
        for side, relay, dst, near, far, col, land in routes(T, topo, rc):
            if relay != core:
                continue
            rid, pid = topo.addr(dst, core)
            m = mask_of(far)
            g.wait_ge(T.sem.ra, len(near))
            g.remote_dma(T.qx[:, land:land + H].bitcast(dt.uint8), T.rq[:, 0:H].bitcast(dt.uint8), T.sem.arr, T.sem.loc, pid, rid, m)
            g.wait_ge(T.sem.rb, len(near))
            g.remote_dma(T.sx[:, land:land + H], T.rs[:, 0:H], T.sem.arr, T.sem.loc, pid, rid, m)
            g.wait_ge(T.sem.loc, 2 * len(far))


def rank_program(g, core, T, topo):
    rank = T.rank_of(core)
    if rank is None:
        relay_program(g, core, T, topo)
        return
    n = len(T.cores)
    first, last = rank == 0, rank == n - 1
    end = first or last
    S, A, CP, ID = T.sem, AluOpType, ActivationFunctionType.Copy, ActivationFunctionType.Identity
    V, C, P, Y = g.vector, g.scalar, g.tensor, g.sync
    pv, pf = [T["pv%d" % b] for b in range(4)], [T.pf0, T.pf1]
    banks = {"a": pf, "b": [T.pl, T.px], "e": [pv[0], pv[2]]}
    lists = {"a": T.pl, "b": T.px}
    hc = H if end else 2 * H
    ring = TC + hc
    wide = {"a": TC - 1, "b": TC - 1, "e": TC + H - 1 if first else ring + 2 * H - 1}
    again = [] if first else ["g_vd", "g_dd", "v_dx"]
    e0, e1 = RUNS["e"]
    back = {r: 2 if r != "e" and RUNS[r][1] - RUNS[r][0] == 8 else 0 for r in RUNS}
    half = {"a": 128, "b": 0}
    out = routes(T, topo, core)
    arrivals = sum(2 * len(q[4]) for nb in (rank - 1, rank + 1) if 0 <= nb < n for q in routes(T, topo, T.cores[nb]) if q[2] == core)
    seen = {}

    def waits(q, *pairs):
        for name in pairs:
            a, _, c = name.partition(":")
            if seen.get((q, a), 0) < int(c or 1):
                seen[q, a] = int(c or 1)
                {"G": g, "V": V, "S": C, "T": P, "Y": Y}[q].wait_ge(S[a], int(c or 1))

    def words(r):
        return slice(16 * RUNS[r][0], 16 * RUNS[r][1])

    def m_of(r, t=0, every=1):
        return T.mt[:, 64 * RUNS[r][0] + t:64 * RUNS[r][1]:every]

    def v_at(t, r):
        return T.vw[:, t, 0:wide[r]].indirect(T.lv[:, RUNS[r][0]:RUNS[r][1]])

    def d_at(t, r):
        return T.dw[:, t, 0:1 + wide[r]].indirect(T.ld[:, RUNS[r][0]:RUNS[r][1]])

    def y_out(q, call, r, o):
        waits(q, "t_o%s%d" % (r, o))
        a, e = RUNS[r]
        for h in range(2):
            call(T.ys[:, 8 * o + a // 4:8 * o + e // 4, h:32:2], banks[r][o][:, back[r] + h:16 * (e - a) + back[r] - 2:4]).then_inc(S["s_y%s%d" % (r, o)], 1)

    def gpsimd(step):
        if step == "part":
            g.iota(T.pi[:], [[0, 1]], 0, 1).then_inc(S.g_p, 1)
        elif step == "eye":
            g.iota(T.dg[:], [[1, 128]], 0, -1, allow_small_or_imprecise_dtypes=True).then_inc(S.g_e, 1)
        elif step == "cols":
            g.iota(T.ic[:, 0:28], [[8, 28]], 1 + H, 0, allow_small_or_imprecise_dtypes=True).then_inc(S.g_c, 1)
            g.iota(T.ic[:, 28:32], [[8, 4]], 1 + (0 if first else ring), 0, allow_small_or_imprecise_dtypes=True).then_inc(S.g_c, 1)
        elif step == "send":
            waits("G", "v_qe")
            codes, planes = [], []
            for side, relay, dst, near, far, col, land in out:
                rid, pid = topo.addr(relay, core)
                to = [DstId(rid=rid, pnc=pid)]
                codes.append(RemoteDMATransfer(dst_ids=to, dma_engine_mask=mask_of(near), remote_sem=S.ra,
                                               src=T.qx[:, col:col + H].bitcast(dt.uint8), dst=T.rq[:, 0:H].bitcast(dt.uint8)))
                planes.append(RemoteDMATransfer(dst_ids=to, dma_engine_mask=mask_of(near), remote_sem=S.rb,
                                                src=T.sx[:, col:col + H], dst=T.rs[:, 0:H]))
            g.remote_dma_fused(codes, local_sem=S.loc)
            g.remote_dma_fused(planes, local_sem=S.loc)
        elif step[0] == "w":
            k = int(step[1])
            g.dma_start(T.wb[:, 4 * TC * k:4 * TC * (k + 1)], T.w[:, 4 * TC * k:4 * TC * (k + 1)]).then_inc(S["d_w%d" % k], 16)
        elif step == "vdup":
            if not first:
                waits("G", "s_va0", "s_va1", "s_va2", "s_va3")
                g.affine_select(T.vw[:, :, ring:ring + 2 * H], T.vw[:, :, 0:2 * H], [[0, 8 * H]], A.is_equal, 0.0, 0, 0).then_inc(S.g_vd, 1)
        elif step == "ddup":
            if not first:
                waits("G", "v_da0", "v_da1", "v_da2", "v_da3")
                g.affine_select(T.dw[:, :, 1 + ring:1 + ring + 2 * H], T.dw[:, :, 1:1 + 2 * H], [[0, 8 * H]], A.is_equal, 0.0, 0, 0).then_inc(S.g_dd, 1)
        elif step[:3] == "add":
            r = step[4]
            waits("G", "v_p%s:4" % r, "s_g%s:4" % r)
            g.dma_start(m_of(r), T.pr[:, words(r), :], accum_op=A.add).then_inc(S["d_m" + r], 16)

    def vector(step):
        t = int(step[-1]) if step[-1].isdigit() else int(step[1]) if step[1:2].isdigit() else None
        if step == "fill":
            V.memset(T.nil[:], 0.0).then_inc(S.v_zt, 1)
            V.memset(T.eye[:], 0.0).then_inc(S.v_eye, 1)
        elif step == "ones":
            waits("V", "v_eye", "g_e")
            V.tensor_scalar(T.eye[:, 4:516:4], T.dg[:], 0.0, None, A.is_equal).then_inc(S.v_one, 1)
        elif step[0] == "u":
            waits("V", "s_u1:2", "s_u%d" % (t - 1))
            c = 2 ** (t - 1)
            V.tensor_copy(T.us[:, :, :, c:2 * c, :], T.us[:, :, :, 0:c, :]).then_inc(S["s_u%d" % t], 1)
        elif step[0] == "r":
            a = half[step[1]]
            waits("V", "t_f" + step[1:])
            V.tensor_scalar(T.fn[:, TC * t + a:TC * t + a + 128], pf[t][:, 0:128], ROUND, -ROUND, A.add, A.add).then_inc(S["s_n" + step[1:]], 1)
        elif step == "bits":
            waits("V", "g_p")
            V.tensor_scalar(T.b0[:], T.pi[:], 1, None, A.bitwise_and).then_inc(S.v_b, 1)
            V.tensor_scalar(T.b1[:], T.pi[:], 1, 6, A.logical_shift_right, A.bitwise_and).then_inc(S.v_b, 1)
        elif step == "m1":
            waits("V", "v_b:2")
            V.tensor_copy(T.m1[:], T.b0[:]).then_inc(S.v_m1, 1)
        elif step == "hs":
            waits("V", "v_m1")
            V.tensor_scalar(T.hs[:], T.b1[:], T.m1[:], None, A.add).then_inc(S.v_hs, 1)
        elif step[:3] == "eye":
            waits("V", "v_one")
            V.quantize_mx(T.qi[:, 128 * t:128 * t + 128], T.si[:, 128 * t:128 * t + 128], T.eye[:, 4 - t:516 - t]).then_inc(S["v_e%d" % t], 1)
        elif step == "qe":
            waits("V", "d_xe:32")
            V.quantize_mx(T.qx[:, X0 - LEAD:X0 + 128], T.sx[:, X0 - LEAD:X0 + 128], T.xt[:, 0:4 * (LEAD + 128)]).then_inc(S.v_qe, 1)
        elif step == "qx":
            waits("V", "d_x:16")
            V.quantize_mx(T.qx[:, X0 + 128:X0 + TC], T.sx[:, X0 + 128:X0 + TC], T.xt[:, 4 * (LEAD + 128):4 * (LEAD + TC)]).then_inc(S.v_qx, 1)
        elif step == "qz":
            waits("V", "s_zt:4")
            V.quantize_mx(T.qz[:], T.sz[:], T.zt[:]).then_inc(S.v_qz, 1)
        elif step == "qu":
            waits("V", "s_u4")
            V.quantize_mx(T.qu[:], T.su[:], T.us[:]).then_inc(S.v_qu, 1)
        elif step[:2] == "qw":
            waits("V", "d_w%d:16" % t)
            V.quantize_mx(T.qw[:, TC * t:TC * t + TC], T.sw[:, TC * t:TC * t + TC], T.wb[:, 4 * TC * t:4 * TC * (t + 1)]).then_inc(S.v_qw, 1)
        elif step == "dl":
            waits("V", "s_p:4")
            V.tensor_tensor(T.dl[:], T.pa[:], T.pb[:], A.add).then_inc(S.v_dl, 1)
        elif step == "nl":
            waits("V", "v_dl")
            V.tensor_scalar(T.nl[:], T.dl[:], -float(CL), float(CL), A.max, A.min).then_inc(S.v_nl, 1)
            V.tensor_scalar(T.dc[:], T.dl[:], -float(CL), float(CL), A.max, A.min).then_inc(S.v_dc, 1)
        elif step == "w":
            waits("V", "v_nl", "s_tab")
            V.tensor_tensor(T.wl[:], T.nl[:], T.tab[:], A.add).then_inc(S.v_wl, 1)
        elif step == "eq":
            waits("V", "v_dc")
            V.tensor_tensor(T.eq[:], T.dc[:], T.dl[:], A.is_equal).then_inc(S.v_eq, 1)
        elif step == "end":
            if end:
                waits("V", "v_wl")
                wl = T.wl[:, 24:28] if last else T.wl[:, 28:32]
                V.tensor_scalar(wl, wl, float(TC) if last else 1.0, None, A.min if last else A.max).then_inc(S.v_we, 1)
        elif step == "lv":
            waits("V", "v_we" if end else "v_wl")
            V.tensor_scalar(T.lv[:], T.wl[:], -1.0, None, A.add).then_inc(S.v_lv, 1)
        elif step == "wz":
            waits("V", "v_we" if end else "v_wl", "v_eq")
            V.tensor_tensor(T.wz[:], T.wl[:], T.eq[:], A.mult).then_inc(S.v_wz, 1)
        elif step == "ld":
            waits("V", "v_wz")
            V.tensor_copy(T.ld[:], T.wz[:]).then_inc(S.v_ld, 1)
        elif step[:2] == "da":
            waits("V", "s_va%d" % t)
            V.tensor_tensor(T.dw[:, t, 1:1 + ROT], T.vw[:, t, 1:1 + ROT], pv[t][:, 0:ROT], A.subtract).then_inc(S["v_da%d" % t], 1)
        elif step[:2] == "db":
            waits("V", "s_vb%d" % t)
            V.tensor_tensor(T.dw[:, t, 1 + ROT:TC], T.vw[:, t, 1 + ROT:TC], pv[t][:, 0:EL - 1], A.subtract).then_inc(S["v_db%d" % t], 1)
        elif step == "fill":
            pass
        elif step[0] == "f":
            a = half[step[1]]
            z = 4 * (128 - a)
            waits("V", "s_n" + step[1:])
            for h in range(2):
                V.tensor_tensor(T.zf[:, z + 4 * t + 2 * h + 1:z + 512:8], pf[t][:, h:128:2], T.fn[:, TC * t + a + h:TC * t + a + 128:2],
                                A.subtract).then_inc(S["v_" + step], 1)
        elif step[0] == "p":
            r = step[2]
            waits("V", "v_ld", "s_z:3", "v_fa0:2", "v_fa1:2", "v_da%d" % t, "v_db%d" % t, *([] if r == "a" else ["v_fb0:2", "v_fb1:2"]))
            waits("V", *(["v_h%d" % t] + again if r == "e" else []))
            V.tensor_tensor(T.pr[:, words(r), t], d_at(t, r), T.zf[:, 32 * RUNS[r][0] + 1:32 * RUNS[r][1]:2], A.mult).then_inc(S["v_pe%d" % t if r == "e" else "v_p" + r], 1)
        elif step == "hx":
            if not first:
                waits("V", "s_h0", "s_h1", "s_h2", "s_h3")
                V.tensor_tensor(T.dw[:, :, ring], T.vw[:, :, 0], T.vw[:, :, ring - 1], A.subtract).then_inc(S.v_dx, 1)
        elif step[0] == "h":
            a = TC if last else TC - 1
            waits("V", "s_h%d" % t)
            V.tensor_tensor(T.dw[:, t, 1 + a:ring], pv[t][:, 128 - (ring - 1 - a):128], T.vw[:, t, a:ring - 1], A.subtract).then_inc(S["v_h%d" % t], 1)
        elif step[:4] == "scan":
            waits("V", "s_z:3", "s_g%d:2" % t, "v_fb0:2", "v_fb1:2")
            V.tensor_tensor_scan(m_of("e", t - 2, 2) if t > 1 else T.tm[:, t, 0:32 * (e1 - e0)], T.zf[:, 32 * e0:32 * e1],
                                 T.gi[:, t, 0:32 * (e1 - e0)], 0.0, A.mult, A.add).then_inc(S["v_s%d" % t], 1)
        elif step[0] == "m":
            waits("V", "v_pe%d" % t, "v_s%d" % (t + 2))
            V.tensor_tensor(m_of("e", t, 4), v_at(t, "e"), T.pr[:, words("e"), t], A.add).then_inc(S.v_me, 1)
        elif step[0] == "c":
            waits("V", "v_s%d" % t, "v_s%d" % (t + 2))
            V.tensor_copy(m_of("e", t, 4), T.tm[:, t, 1:32 * (e1 - e0):2]).then_inc(S.v_me, 1)
        elif step[0] == "q":
            r = step[1]
            waits("V", "v_me:2" if r == "e" else "d_m%s:16" % r)
            a, e = 16 * RUNS[r][0], 16 * RUNS[r][1] + (2 if r == "e" else 0)
            V.quantize_mx(T.qm[:, a:e], T.sm[:, a:e], T.mt[:, 4 * a:4 * e]).then_inc(S["v_" + step], 1)
        elif step[0] == "y":
            y_out("V", V.tensor_copy, step[1], t)

    def mm(o, cols, lq, ls, a, rq, rs, c, start, stop):
        return P.matmul_mx(o[:, 0:cols], lq[:, a:a + 128], ls[:, a:a + 128], rq[:, c:c + cols], rs[:, c:c + cols], start, stop)

    def tensor(step):
        t = int(step[-1]) if step[-1].isdigit() else None
        if step[:2] == "va":
            waits("T", "v_qx", "v_db%d" % t)
            mm(pv[t], ROT, T.qi, T.si, 128 * t, T.qx, T.sx, X0 + EL, True, True).then_inc(S["t_va%d" % t], 1)
        elif step[:2] == "vb":
            waits("T", "v_qe", "v_e%d" % t)
            mm(pv[t], 128, T.qi, T.si, 128 * t, T.qx, T.sx, X0, True, True).then_inc(S["t_vb%d" % t], 1)
        elif step[0] == "l":
            waits("T", "v_qz", "v_qe", *(["v_qx"] if step == "la" else []))
            for h in range(4):
                r = mm(lists[step[1]], 128, T.qz, T.sz, 12 - 4 * h, T.qx, T.sx, X0 - LEAD + half[step[1]] + 2 * h, h == 0, h == 3)
            r.then_inc(S["t_" + step], 1)
        elif step[0] == "f":
            waits("T", "v_qu", "v_qe", "v_qx", *(["v_fa%d:2" % t] if step[1] == "b" else []))
            mm(pf[t], 128, T.qu, T.su, 128 * t, T.qx, T.sx, X0 + half[step[1]], True, True).then_inc(S["t_" + step], 1)
        elif step[0] == "h":
            waits("T", "arr:%d" % arrivals, "v_da%d" % t)
            mm(pv[t], 128, T.qi, T.si, 128 * t, T.qx, T.sx, X0 + ring - 128, True, True).then_inc(S["t_h%d" % t], 1)
        else:
            r = step[1]
            waits("T", "v_qw:2", "v_fb0:2", "v_fb1:2", "s_p:4", "v_qe2" if r == "e" else "v_q" + r, *(["v_qa"] if back[r] else []))
            a = 16 * RUNS[r][0] - back[r]
            cols = max(128, 16 * (RUNS[r][1] - RUNS[r][0]) - 2)
            for o in range(2):
                mm(banks[r][o], cols, T.qw, T.sw, 128 * o, T.qm, T.sm, a, True, False)
                mm(banks[r][o], cols, T.qw, T.sw, 256 + 128 * o, T.qm, T.sm, a + 2, False, True).then_inc(S["t_o%s%d" % (r, o)], 1)

    def store(q, call, step, sem):
        if step[0] == "w":
            k = int(step[1])
            call(T.wb[:, 4 * TC * k:4 * TC * (k + 1)], T.w[:, 4 * TC * k:4 * TC * (k + 1)]).then_inc(S["d_w%d" % k], 16)
            return
        r, o = step[1], int(step[2])
        a, e = RUNS[r]
        if r != "e":
            waits(q, "s_y%s%d:2" % (r, o))
            call(T.y[:, TC * o + H + 8 * a:TC * o + H + 8 * e], T.ys[:, 8 * o + a // 4:8 * o + e // 4, :]).then_inc(sem, 16)
        elif o < 2:
            waits(q, "s_ye%d:2" % o)
            call(T.y[:, TC * o:TC * o + H], T.ys[:, 8 * o + 7, :]).then_inc(sem, 16)
        elif o < 4:
            waits(q, "s_ye%d:2" % (o - 2))
            call(T.y[:, TC * (o - 2) + H + 8 * a:TC * (o - 1)], T.ys[:, 8 * (o - 2) + a // 4:8 * (o - 2) + 7, :]).then_inc(sem, 16)
        else:
            waits(q, "s_ye0:2", "s_ye1:2")
            call(T.y[:, TC - H:TC + H], T.ys[:, 6:16:9, :]).then_inc(sem, 16)

    def scalar(step):
        t = int(step[-1]) if step[-1].isdigit() else int(step[1]) if step[1:2].isdigit() else None
        if step == "nil":
            waits("S", "v_zt")
            for i in range(4):
                C.activation(T.zt[:, :, 4 * i:4 * i + 4, :], T.nil[:, 0:144], CP).then_inc(S.s_nil, 1)
        elif step == "zeros":
            waits("S", "v_zt")
            C.activation(T.dw[:, :, 0:TC + 1:TC] if last else T.dw[:, :, 0], T.nil[:, 0:8 if last else 4], CP).then_inc(S.s_z, 1)
            C.activation(T.mt[:, 2048:2056], T.nil[:, 0:8], CP).then_inc(S.s_z, 1)
            C.activation(T.zf[:, 32 * e0:32 * e1:2], T.nil[:, 0:16 * (e1 - e0)], CP).then_inc(S.s_z, 1)
        elif step == "zt":
            waits("S", "s_nil:4", "d_u:16")
            for k in range(2):
                for e in range(2):
                    C.activation(T.zt[:, 0:8, 12 + 2 * k + e, :], T.ub[:, k, :, :], CP).then_inc(S.s_zt, 1)
        elif step == "u1":
            waits("S", "d_u:16")
            for q in range(2):
                C.activation(T.us[:, :, :, q, :], T.ub[:], CP).then_inc(S.s_u1, 1)
        elif step[0] == "u":
            waits("S", "s_u1:2", "s_u%d" % (t - 1))
            c = 2 ** (t - 1)
            C.activation(T.us[:, :, :, c:2 * c, :], T.us[:, :, :, 0:c, :], CP).then_inc(S["s_u%d" % t], 1)
        elif step == "m0":
            waits("S", "v_m1")
            C.activation(T.m0[:], T.m1[:], CP, 1.0, -1.0).then_inc(S.s_m0, 1)
        elif step == "tab":
            waits("S", "v_hs", "g_c:2")
            C.activation(T.tab[:], T.ic[:], ID, T.hs[:]).then_inc(S.s_tab, 1)
        elif step[:2] == "va":
            waits("S", "t_va%d" % t)
            C.activation(T.vw[:, t, 0:ROT], pv[t][:, 0:ROT], CP).then_inc(S["s_va%d" % t], 1)
        elif step[:2] == "vb":
            waits("S", "t_vb%d" % t)
            C.activation(T.vw[:, t, ROT:TC], pv[t][:, 0:EL], CP).then_inc(S["s_vb%d" % t], 1)
        elif step[0] == "l":
            waits("S", "t_" + step, "s_m0")
            z = (128 - half[step[1]]) // 8
            C.activation(T.pa[:, z:z + 16], lists[step[1]][:, LEAD:128:8], CP, 0.0, T.m0[:]).then_inc(S.s_p, 1)
            C.activation(T.pb[:, z:z + 16], lists[step[1]][:, LEAD + 1:128:8], CP, 0.0, T.m1[:]).then_inc(S.s_p, 1)
        elif step[0] == "r":
            a = half[step[1]]
            waits("S", "t_f" + step[1:])
            C.activation(T.r1[:, TC * t + a:TC * t + a + 128], pf[t][:, 0:128], CP, ROUND).then_inc(S["s_" + step], 1)
        elif step[0] == "n":
            a = TC * t + half[step[1]]
            waits("S", "s_r" + step[1:])
            C.activation(T.fn[:, a:a + 128], T.r1[:, a:a + 128], CP, -ROUND).then_inc(S["s_" + step], 1)
        elif step[0] == "g" and step[2] != "e":
            waits("S", "v_lv", "s_va%d" % t, "s_vb%d" % t)
            C.activation(m_of(step[2], t, 4), v_at(t, step[2]), CP).then_inc(S["s_g" + step[2]], 1)
        elif step[0] == "g":
            waits("S", "v_lv", "s_va%d" % t, "s_vb%d" % t, "s_h%d" % t, *again[:1])
            C.activation(T.gi[:, t, 1:32 * (e1 - e0):2], v_at(t, "e"), CP).then_inc(S["s_g%d" % t], 1)
        elif step[0] == "e":
            waits("S", "v_ld", "s_z:3", "v_da%d" % t, "v_db%d" % t, "v_h%d" % t, *again)
            C.activation(T.gi[:, t, 0:32 * (e1 - e0):2], d_at(t, "e"), CP).then_inc(S["s_g%d" % t], 1)
        elif step[0] == "h":
            waits("S", "t_h%d" % t)
            C.activation(T.vw[:, t, TC:ring], pv[t][:, 128 - hc:128], CP).then_inc(S["s_h%d" % t], 1)
        elif step[0] == "y":
            y_out("S", lambda a, b: C.activation(a, b, CP), step[1], t)
        elif step[0] == "s":
            store("S", C.dma_start, step, S.st2)

    C.dma_start(T.xt[:, 4 * (LEAD + EL):4 * (LEAD + 128)], T.x[:, 0:512 - 4 * EL]).then_inc(S.d_xe, 16)
    Y.dma_start(T.ub[:], T.u[:, 0:64]).then_inc(S.d_u, 16)
    Y.dma_start(T.xt[:, 0:4 * (LEAD + EL)], T.x[:, 4 * (ROT - LEAD):4 * TC]).then_inc(S.d_xe, 16)
    Y.dma_start(T.xt[:, 4 * (LEAD + 128):4 * (LEAD + TC)], T.x[:, 512 - 4 * EL:4 * ROT]).then_inc(S.d_x, 16)
    for q, run in (("G", gpsimd), ("V", vector), ("T", tensor), ("S", scalar), ("Y", lambda step: store("Y", Y.dma_start, step, S.st1))):
        for step in ORDER[q].split():
            run(step)
    waits("G", "loc:%d" % sum(2 * len(q[3]) for q in out))
    waits("S", "st2:%d" % (16 * sum(step[0] == "s" for step in ORDER["S"].split())))
    waits("Y", "st1:%d" % (16 * sum(step[0] == "s" for step in ORDER["Y"].split())))
